import numpy as np
import ml_dtypes


def mxq(x, axis, fmt="e4m3"):
    dtype, down = {"e4m3": (ml_dtypes.float8_e4m3fn, 7), "e5m2": (ml_dtypes.float8_e5m2, 14)}[fmt]
    v = np.moveaxis(np.asarray(x, np.float32).astype(ml_dtypes.bfloat16).astype(np.float64), axis, -1)
    blocks = v.reshape(v.shape[:-1] + (-1, 32))
    amax = np.abs(blocks).max(-1, keepdims=True)
    byte = np.maximum(np.where(amax > 0, np.frexp(amax)[1] - 1 + 127, 0) - down, 1)
    scale = np.exp2(byte - 127.0)
    codes = (blocks / scale).astype(np.float32).astype(dtype).astype(np.float64)
    return np.moveaxis((codes * scale).reshape(v.shape), -1, axis)


WIDE = False


def mx_kscale(k):
    if not WIDE:
        return np.ones(k)
    levels = np.array([10, -10, 5, -5, 0])
    if k % 512:
        return np.exp2(np.random.permutation(np.resize(levels, k // 32))).repeat(32)
    a = np.empty((k // 512, 16))
    for p in range(k // 512):
        a[p, :8] = np.random.permutation(np.resize(levels, 8))
        for g in range(8):
            far = levels[np.abs(levels - a[p, g]) >= 10]
            a[p, g + 8] = far[np.random.randint(len(far))]
    return np.exp2(a.ravel()).repeat(32)


def f64(x):
    return np.asarray(x).astype(np.float64)


def striped(idx):
    return np.tile(idx.reshape(-1, 16).T, (8, 1)).astype(np.uint16)


def unstriped(offs):
    return offs[:16].T.reshape(-1).astype(np.int64)


def pack_weight(w):
    k, n = w.shape
    w = f64(np.asarray(w, np.float32).astype(ml_dtypes.bfloat16)).reshape(k // 32, 32, n)
    amax = np.abs(w).max(1)
    byte = np.clip(np.where(amax > 0, np.frexp(amax)[1] - 1 + 127 - 7, 1), 1, 254)
    scaled = (w * np.exp2(127.0 - byte)[:, None, :]).reshape(k, n).astype(np.float32)
    words = np.ascontiguousarray(scaled.reshape(k // 512, 128, 4, n).transpose(0, 1, 3, 2)).astype(ml_dtypes.float8_e4m3fn).view(np.uint8)
    return words, np.ascontiguousarray(byte.astype(np.uint8).reshape(k // 512, 16, n))


def unpack_weight(words, scales):
    g, p, n, _ = words.shape
    vals = np.ascontiguousarray(words).view(ml_dtypes.float8_e4m3fn).astype(np.float64) * np.repeat(np.exp2(scales.astype(np.float64) - 127.0), 8, axis=1)[..., None]
    return vals.transpose(0, 1, 3, 2).reshape(g * 512, n)


def planes(y):
    n, m = y.shape
    v = y.astype(np.float32).astype(ml_dtypes.bfloat16).astype(np.float64).reshape(n // 32, 32, m)
    top = np.abs(v).max(1)
    byte = np.clip(np.where(top > 0, np.frexp(top)[1] - 1 + 127 - 7, 1), 1, 254)
    codes = (v * np.exp2(127.0 - byte)[:, None, :]).reshape(n, m).astype(np.float32).astype(ml_dtypes.float8_e4m3fn).view(np.uint8)
    words = codes.reshape(n // 512, 128, 4, m).transpose(0, 1, 3, 2)
    return np.ascontiguousarray(words), np.ascontiguousarray(byte.astype(np.uint8).reshape(n // 512, 16, m))


K, T, S, N = 1024, 4096, 1024, 512
P = 2 ** 7


def setup_inputs():
    n = np.random.standard_normal
    s = mx_kscale(K)[:, None]
    packed_xT = pack_weight(n((K, T)) * s)
    return {
        "x_words": packed_xT[0],
        "x_scales": packed_xT[1],
        "w1": (n((K, N)) / np.sqrt(K) / s).astype(np.float32),
        "gain": (np.tile(np.random.uniform(0.5, 1.5, T), (P, 1))).astype(np.float32),
        "shift": (np.tile(0.5 * np.random.standard_normal(T), (P, 1))).astype(np.float32),
        "wsum": (n((N, 1))).astype(np.float32),
        "offs": striped(np.random.permutation(T)[:S]),
    }


def reference(x_words, x_scales, w1, gain, shift, wsum, offs):
    xq = unpack_weight(x_words, x_scales)[:, unstriped(offs)]
    y = mxq(f64(w1), 0, "e4m3").T @ xq
    g = f64(gain)[:1][:, unstriped(offs)]
    t = f64(shift)[:1][:, unstriped(offs)]
    out_0 = y * g + f64(wsum) * t
    return (out_0,) + planes(out_0)

@@ -1,0 +1,168 @@
+from contextlib import ExitStack
+
+import concourse.mybir as mybir
+from concourse.masks import make_identity
+
+K, T, S, N = 1024, 4096, 1024, 512
+FLOPS = 2 * K * N * S
+BYTES = K * T + K * T // 32 + 4 * K * N + 2 * 4 * T + 4 * N + 2 * 128 * S // 16 + 4 * N * S + N * S + N * S // 32
+
+F32 = mybir.dt.float32
+BF16 = mybir.dt.bfloat16
+I32 = mybir.dt.int32
+U32 = mybir.dt.uint32
+U16 = mybir.dt.uint16
+U8 = mybir.dt.uint8
+FP8X4 = mybir.dt.float8_e4m3fn_x4
+MULT = mybir.AluOpType.mult
+ADD = mybir.AluOpType.add
+COPY = mybir.ActivationFunctionType.Copy
+
+P = 128
+PACK = 4
+PASSES = K // (P * PACK)
+BLOCKS = S // P
+HALF = S // 2
+CHUNK = 2 * P
+GAIN_ROW = 126
+ROW_STEP = 1
+SHIFT_ROW = GAIN_ROW + ROW_STEP
+
+
+def interleave(copy, dst, src):
+    copy(out=dst.rearrange("p (c i) r -> p c r i", i=4), in_=src.rearrange("p r (c i) -> p c r i", i=4))
+
+
+def tile_picked_zdq_linnone_po_kernel(
+    tc, x_words, x_scales, w1, gain, shift, wsum, offs, out_0, out_1, out_2
+):
+    nc = tc.nc
+    with ExitStack() as ctx:
+        keep = ctx.enter_context(tc.tile_pool(name="keep", bufs=1))
+        psum = ctx.enter_context(tc.psum_pool(name="psum", bufs=1))
+
+        offsets = keep.tile([P, S // 16], U16, name="offsets")
+        nc.sync.dma_start(offsets[:], offs)
+
+        ident = keep.tile([P, P], F32, name="ident")
+        make_identity(nc, ident[:])
+
+        scale_table = keep.tile([P, T], U8, name="scale_table")
+        nc.vector.memset(scale_table[:].bitcast(I32), 0)
+        row_table = keep.tile([P, T], F32, name="row_table", tag="words1")
+        nc.vector.memset(row_table[:GAIN_ROW, : T // 2], 0.0)
+        nc.gpsimd.memset(row_table[:GAIN_ROW, T // 2 :], 0.0)
+        nc.sync.dma_start(row_table[GAIN_ROW : GAIN_ROW + 1, :], gain[0:1, :])
+        nc.sync.dma_start(row_table[SHIFT_ROW : SHIFT_ROW + 1, :], shift[0:1, :])
+        wsum_cols = keep.tile([P, PACK], F32, name="wsum_cols", tag="words0")
+        nc.sync.dma_start(wsum_cols[:], wsum.rearrange("(p t) o -> p (t o)", t=PACK))
+
+        w_raw = []
+        for o in range(PASSES):
+            raw = keep.tile([P, PACK, N], F32, name="w_raw%d" % o)
+            nc.sync.dma_start(raw[:], w1[512 * o : 512 * (o + 1), :].rearrange("(p r) m -> p r m", r=PACK))
+            w_raw.append(raw)
+        for q in range(4):
+            if q < 2:
+                nc.sync.dma_start(
+                    scale_table[32 * q : 32 * q + 8, :].bitcast(I32), x_scales[:, 4 * q : 4 * q + 4, :].bitcast(I32)
+                )
+            else:
+                for o in range(PASSES):
+                    first = 32 * q + 4 * o
+                    nc.sync.dma_start(
+                        scale_table[first : first + 4, :].bitcast(I32), x_scales[o, 4 * q : 4 * q + 4, :].bitcast(I32)
+                    )
+        bank = psum.tile([P, PACK, P], F32, name="wsum_bank", tag="bank2")
+        for t in range(PACK):
+            nc.tensor.transpose(bank[:, t, :], wsum_cols[:, t : t + 1].to_broadcast([P, P]), ident[:])
+        wsum_row = keep.tile([P, N], F32, name="wsum_row")
+        nc.scalar.copy(wsum_row[:], bank[:].rearrange("p t m -> p (t m)"))
+
+        picked_rows = keep.tile([P, S], F32, name="picked_rows")
+        nc.vector.tensor_copy(picked_rows[:], row_table[:].indirect(offsets[:]))
+
+        word_table = []
+        for o in range(PASSES):
+            table = keep.tile([P, T], U32, name="word_table%d" % o, tag="words%d" % o)
+            nc.sync.dma_start(table[:].bitcast(I32), x_words[o].rearrange("p c r -> p (c r)").bitcast(I32))
+            word_table.append(table)
+        x_planes = keep.tile([P, S], U8, name="x_planes", align_bytes=64)
+        nc.vector.tensor_copy(x_planes[:], scale_table[:].indirect(offsets[:]))
+
+        w_codes, w_planes = [], []
+        for o in range(PASSES):
+            grouped = keep.tile([P, N, PACK], BF16, name="w_grouped%d" % o, align_bytes=64)
+            interleave(nc.scalar.copy, grouped[:], w_raw[o][:])
+            codes = keep.tile([P, N], U32, name="w_codes%d" % o, align_bytes=64)
+            plane = keep.tile([P, N], U8, name="w_plane%d" % o, align_bytes=64)
+            nc.vector.quantize_mx(
+                out=codes[:].bitcast(FP8X4), scales=plane[:], in_=grouped[:].rearrange("p m r -> p (m r)")
+            )
+            w_codes.append(codes)
+            w_planes.append(plane)
+
+        factors = keep.tile([P, BLOCKS, 2], F32, name="factors")
+        for g in range(BLOCKS // 4):
+            bank = psum.tile([P, 4, P], F32, name="turned_rows", tag="bank%d" % g)
+            for i in range(4):
+                b = 4 * g + i
+                nc.tensor.transpose(bank[:, i, :], picked_rows[:, P * b : P * (b + 1)], ident[:])
+            nc.scalar.copy(factors[:, 4 * g : 4 * g + 4, :], bank[:, :, GAIN_ROW::ROW_STEP])
+
+        offset_terms = []
+        for b in range(BLOCKS):
+            term = keep.tile([P, N], F32, name="offset_term%d" % b)
+            nc.scalar.activation(term[:], wsum_row[:], COPY, scale=factors[:, b, 1:2])
+            offset_terms.append(term)
+
+        sums = [psum.tile([P, N], F32, name="sums%d" % b, tag="bank%d" % b) for b in range(BLOCKS)]
+        for o in range(PASSES):
+            width = S if o == 0 else HALF
+            for first in range(0, S, width):
+                codes = keep.tile([P, width], U32, name="x_codes%d_%d" % (o, first), align_bytes=64)
+                nc.vector.tensor_copy(
+                    codes[:], word_table[o][:].indirect(offsets[:, first // 16 : (first + width) // 16])
+                )
+                for c in range(0, width, P):
+                    nc.tensor.matmul_mx(
+                        out=sums[(first + c) // P][:],
+                        lhsT=codes[:, c : c + P].bitcast(FP8X4),
+                        lhsT_scale=x_planes[4 * o :, first + c : first + c + P],
+                        rhs=w_codes[o][:].bitcast(FP8X4),
+                        rhs_scale=w_planes[o][:],
+                        start=(o == 0),
+                        stop=(o == PASSES - 1),
+                    )
+
+        out_rows = out_0.rearrange("(p t) j -> p t j", t=PACK)
+        out_words = out_1[0].rearrange("p j r -> p (j r)").bitcast(I32)
+        out_plane = keep.tile([P, S], U8, name="out_plane", align_bytes=64)
+        for chunk in range(S // CHUNK):
+            cols = slice(CHUNK * chunk, CHUNK * (chunk + 1))
+            result = keep.tile([P, PACK, CHUNK], F32, name="result%d" % chunk)
+            for i in range(CHUNK // P):
+                b = CHUNK // P * chunk + i
+                by_token = keep.tile([P, PACK, P], F32, name="by_token%d" % b)
+                nc.vector.scalar_tensor_tensor(
+                    by_token[:],
+                    sums[b][:].rearrange("j (p t) -> j t p", t=PACK),
+                    factors[:, b, 0:1],
+                    offset_terms[b][:].rearrange("j (t p) -> j t p", t=PACK),
+                    MULT,
+                    ADD,
+                )
+                turned = psum.tile([P, PACK, P], F32, name="turned%d" % b, tag="bank%d" % b)
+                for t in range(PACK):
+                    nc.tensor.transpose(turned[:, t, :], by_token[:, t, :], ident[:])
+                nc.scalar.copy(result[:, :, P * i : P * (i + 1)], turned[:])
+            nc.sync.dma_start(out_rows[:, :, cols], result[:])
+            rounded = keep.tile([P, CHUNK, PACK], BF16, name="rounded%d" % chunk, align_bytes=64)
+            interleave(nc.scalar.copy if chunk % 2 == 0 else nc.vector.tensor_copy, rounded[:], result[:])
+            codes = keep.tile([P, CHUNK], U32, name="out_codes%d" % chunk, align_bytes=64)
+            nc.vector.quantize_mx(
+                out=codes[:].bitcast(FP8X4), scales=out_plane[:, cols], in_=rounded[:].rearrange("p j r -> p (j r)")
+            )
+            nc.sync.dma_start(out_words[:, cols], codes[:].bitcast(I32))
+        for q in range(4):
+            nc.sync.dma_start(out_2[0, 4 * q : 4 * q + 4, :].bitcast(I32), out_plane[32 * q : 32 * q + 4, :].bitcast(I32))

@@ -24,9 +24,8 @@ PASSES = K // (P * PACK)
 BLOCKS = S // P
 HALF = S // 2
 CHUNK = 2 * P
-GAIN_ROW = 126
-ROW_STEP = 1
-SHIFT_ROW = GAIN_ROW + ROW_STEP
+GAIN_ROW = P - 2
+SHIFT_ROW = P - 1
 
 
 def interleave(copy, dst, src):
@@ -44,49 +43,33 @@ def tile_picked_zdq_linnone_po_kernel(
         offsets = keep.tile([P, S // 16], U16, name="offsets")
         nc.sync.dma_start(offsets[:], offs)
 
-        ident = keep.tile([P, P], F32, name="ident")
-        make_identity(nc, ident[:])
-
         scale_table = keep.tile([P, T], U8, name="scale_table")
         nc.vector.memset(scale_table[:].bitcast(I32), 0)
-        row_table = keep.tile([P, T], F32, name="row_table", tag="words1")
+        zero = keep.tile([P, 1], F32, name="zero", tag="words0", align_bytes=64)
+        nc.gpsimd.memset(zero[:], 0.0)
+        ident = keep.tile([P, P], F32, name="ident")
+        make_identity(nc, ident[:])
+        row_table = keep.tile([P, T], F32, name="row_table")
         nc.vector.memset(row_table[:GAIN_ROW, : T // 2], 0.0)
-        nc.gpsimd.memset(row_table[:GAIN_ROW, T // 2 :], 0.0)
+        nc.scalar.copy(row_table[:GAIN_ROW, T // 2 :], zero[:GAIN_ROW, :].to_broadcast([GAIN_ROW, T // 2]))
         nc.sync.dma_start(row_table[GAIN_ROW : GAIN_ROW + 1, :], gain[0:1, :])
         nc.sync.dma_start(row_table[SHIFT_ROW : SHIFT_ROW + 1, :], shift[0:1, :])
-        wsum_cols = keep.tile([P, PACK], F32, name="wsum_cols", tag="words0")
+        wsum_cols = keep.tile([P, PACK], F32, name="wsum_cols")
         nc.sync.dma_start(wsum_cols[:], wsum.rearrange("(p t) o -> p (t o)", t=PACK))
 
         w_raw = []
         for o in range(PASSES):
-            raw = keep.tile([P, PACK, N], F32, name="w_raw%d" % o)
+            raw = keep.tile([P, PACK, N], F32, name="w_raw%d" % o, tag=("words1", "w_raw1")[o], align_bytes=64)
             nc.sync.dma_start(raw[:], w1[512 * o : 512 * (o + 1), :].rearrange("(p r) m -> p r m", r=PACK))
             w_raw.append(raw)
         for q in range(4):
-            if q < 2:
-                nc.sync.dma_start(
-                    scale_table[32 * q : 32 * q + 8, :].bitcast(I32), x_scales[:, 4 * q : 4 * q + 4, :].bitcast(I32)
-                )
-            else:
-                for o in range(PASSES):
-                    first = 32 * q + 4 * o
-                    nc.sync.dma_start(
-                        scale_table[first : first + 4, :].bitcast(I32), x_scales[o, 4 * q : 4 * q + 4, :].bitcast(I32)
-                    )
-        bank = psum.tile([P, PACK, P], F32, name="wsum_bank", tag="bank2")
-        for t in range(PACK):
-            nc.tensor.transpose(bank[:, t, :], wsum_cols[:, t : t + 1].to_broadcast([P, P]), ident[:])
-        wsum_row = keep.tile([P, N], F32, name="wsum_row")
-        nc.scalar.copy(wsum_row[:], bank[:].rearrange("p t m -> p (t m)"))
+            queue = nc.sync if q % 2 == 0 else nc.gpsimd
+            queue.dma_start(
+                scale_table[32 * q : 32 * q + 8, :].bitcast(I32), x_scales[:, 4 * q : 4 * q + 4, :].bitcast(I32)
+            )
 
         picked_rows = keep.tile([P, S], F32, name="picked_rows")
         nc.vector.tensor_copy(picked_rows[:], row_table[:].indirect(offsets[:]))
-
-        word_table = []
-        for o in range(PASSES):
-            table = keep.tile([P, T], U32, name="word_table%d" % o, tag="words%d" % o)
-            nc.sync.dma_start(table[:].bitcast(I32), x_words[o].rearrange("p c r -> p (c r)").bitcast(I32))
-            word_table.append(table)
         x_planes = keep.tile([P, S], U8, name="x_planes", align_bytes=64)
         nc.vector.tensor_copy(x_planes[:], scale_table[:].indirect(offsets[:]))
 
@@ -102,67 +85,95 @@ def tile_picked_zdq_linnone_po_kernel(
             w_codes.append(codes)
             w_planes.append(plane)
 
-        factors = keep.tile([P, BLOCKS, 2], F32, name="factors")
+        word_table = []
+        for o in range(PASSES):
+            table = keep.tile([P, T], U32, name="word_table%d" % o, tag="words%d" % o, align_bytes=64)
+            nc.sync.dma_start(table[:].bitcast(I32), x_words[o].rearrange("p c r -> p (c r)").bitcast(I32))
+            word_table.append(table)
+
+        factors = keep.tile([P, BLOCKS, 2], F32, name="factors", tag="w_raw1", align_bytes=64)
         for g in range(BLOCKS // 4):
             bank = psum.tile([P, 4, P], F32, name="turned_rows", tag="bank%d" % g)
             for i in range(4):
                 b = 4 * g + i
                 nc.tensor.transpose(bank[:, i, :], picked_rows[:, P * b : P * (b + 1)], ident[:])
-            nc.scalar.copy(factors[:, 4 * g : 4 * g + 4, :], bank[:, :, GAIN_ROW::ROW_STEP])
-
-        offset_terms = []
-        for b in range(BLOCKS):
-            term = keep.tile([P, N], F32, name="offset_term%d" % b)
-            nc.scalar.activation(term[:], wsum_row[:], COPY, scale=factors[:, b, 1:2])
-            offset_terms.append(term)
-
+            nc.scalar.copy(factors[:, 4 * g : 4 * g + 4, :], bank[:, :, GAIN_ROW:])
+        shift_rows = keep.tile([P, S], F32, name="shift_rows")
+        for g in range(BLOCKS // 4):
+            bank = psum.tile([P, 4, P], F32, name="spread_shift", tag="bank%d" % (2 + g))
+            for i in range(4):
+                nc.tensor.transpose(bank[:, i, :], factors[:, 4 * g + i, 1:2].to_broadcast([P, P]), ident[:])
+            nc.scalar.copy(shift_rows[:, HALF * g : HALF * (g + 1)], bank[:].rearrange("p i j -> p (i j)"))
         sums = [psum.tile([P, N], F32, name="sums%d" % b, tag="bank%d" % b) for b in range(BLOCKS)]
-        for o in range(PASSES):
-            width = S if o == 0 else HALF
-            for first in range(0, S, width):
-                codes = keep.tile([P, width], U32, name="x_codes%d_%d" % (o, first), align_bytes=64)
-                nc.vector.tensor_copy(
-                    codes[:], word_table[o][:].indirect(offsets[:, first // 16 : (first + width) // 16])
+
+        def gather_words(o, first, width):
+            codes = keep.tile([P, width], U32, name="x_codes%d_%d" % (o, first), align_bytes=64)
+            nc.vector.tensor_copy(codes[:], word_table[o][:].indirect(offsets[:, first // 16 : (first + width) // 16]))
+            return codes
+
+        def multiply(o, codes, first, width):
+            for c in range(0, width, P):
+                nc.tensor.matmul_mx(
+                    out=sums[(first + c) // P][:],
+                    lhsT=codes[:, c : c + P].bitcast(FP8X4),
+                    lhsT_scale=x_planes[4 * o :, first + c : first + c + P],
+                    rhs=w_codes[o][:].bitcast(FP8X4),
+                    rhs_scale=w_planes[o][:],
+                    start=(o == 0),
+                    stop=(o == PASSES - 1),
                 )
-                for c in range(0, width, P):
-                    nc.tensor.matmul_mx(
-                        out=sums[(first + c) // P][:],
-                        lhsT=codes[:, c : c + P].bitcast(FP8X4),
-                        lhsT_scale=x_planes[4 * o :, first + c : first + c + P],
-                        rhs=w_codes[o][:].bitcast(FP8X4),
-                        rhs_scale=w_planes[o][:],
-                        start=(o == 0),
-                        stop=(o == PASSES - 1),
-                    )
 
         out_rows = out_0.rearrange("(p t) j -> p t j", t=PACK)
+        results = [keep.tile([P, PACK, CHUNK], F32, name="result%d" % c) for c in range(S // CHUNK)]
+
+        def finish(b):
+            scaled = keep.tile([P, PACK, P], F32, name="scaled%d" % b)
+            nc.scalar.activation(
+                scaled[:], sums[b][:].rearrange("j (p t) -> j t p", t=PACK), COPY, scale=factors[:, b, 0:1]
+            )
+            turned = psum.tile([P, PACK, P], F32, name="turned%d" % b, tag="bank%d" % b)
+            for t in range(PACK):
+                nc.tensor.transpose(turned[:, t, :], scaled[:, t, :], ident[:])
+            chunk, i = divmod(b, CHUNK // P)
+            nc.vector.tensor_tensor(
+                results[chunk][:, :, P * i : P * (i + 1)], turned[:], offset_terms[b // 4][:, :, P * (b % 4) : P * (b % 4 + 1)], ADD
+            )
+            if i == CHUNK // P - 1:
+                nc.sync.dma_start(out_rows[:, :, CHUNK * chunk : CHUNK * (chunk + 1)], results[chunk][:])
+
+        for h in range(2):
+            multiply(0, gather_words(0, HALF * h, HALF), HALF * h, HALF)
+        offset_terms = []
+        for h in range(2):
+            term = keep.tile([P, PACK, HALF], F32, name="term%d" % h, tag=("term0", "words0")[h], align_bytes=64)
+            rows = shift_rows[:, HALF * h : HALF * (h + 1)]
+            for t in range(PACK):
+                if h == 0:
+                    nc.scalar.activation(term[:, t, :], rows, COPY, scale=wsum_cols[:, t : t + 1])
+                else:
+                    nc.vector.tensor_scalar(term[:, t, :], rows, wsum_cols[:, t : t + 1], None, MULT)
+            offset_terms.append(term)
+        last = [gather_words(1, HALF * h, HALF) for h in range(2)]
+        multiply(1, last[0], 0, HALF)
+        for b in range(2):
+            finish(b)
+        multiply(1, last[1], HALF, HALF)
+        for b in range(2, BLOCKS):
+            finish(b)
+
         out_words = out_1[0].rearrange("p j r -> p (j r)").bitcast(I32)
         out_plane = keep.tile([P, S], U8, name="out_plane", align_bytes=64)
-        for chunk in range(S // CHUNK):
-            cols = slice(CHUNK * chunk, CHUNK * (chunk + 1))
-            result = keep.tile([P, PACK, CHUNK], F32, name="result%d" % chunk)
-            for i in range(CHUNK // P):
-                b = CHUNK // P * chunk + i
-                by_token = keep.tile([P, PACK, P], F32, name="by_token%d" % b)
-                nc.vector.scalar_tensor_tensor(
-                    by_token[:],
-                    sums[b][:].rearrange("j (p t) -> j t p", t=PACK),
-                    factors[:, b, 0:1],
-                    offset_terms[b][:].rearrange("j (t p) -> j t p", t=PACK),
-                    MULT,
-                    ADD,
-                )
-                turned = psum.tile([P, PACK, P], F32, name="turned%d" % b, tag="bank%d" % b)
-                for t in range(PACK):
-                    nc.tensor.transpose(turned[:, t, :], by_token[:, t, :], ident[:])
-                nc.scalar.copy(result[:, :, P * i : P * (i + 1)], turned[:])
-            nc.sync.dma_start(out_rows[:, :, cols], result[:])
-            rounded = keep.tile([P, CHUNK, PACK], BF16, name="rounded%d" % chunk, align_bytes=64)
-            interleave(nc.scalar.copy if chunk % 2 == 0 else nc.vector.tensor_copy, rounded[:], result[:])
-            codes = keep.tile([P, CHUNK], U32, name="out_codes%d" % chunk, align_bytes=64)
+        for h in range(2):
+            copy = (nc.scalar.copy, nc.vector.tensor_copy)[h]
+            rounded = keep.tile([P, HALF, PACK], BF16, name="rounded%d" % h, tag=("w_raw1", "rounded1")[h], align_bytes=64)
+            for c in range(2):
+                interleave(copy, rounded[:, CHUNK * c : CHUNK * (c + 1), :], results[2 * h + c][:])
+            codes = keep.tile([P, HALF], U32, name="out_codes%d" % h, align_bytes=64)
+            cols = slice(HALF * h, HALF * (h + 1))
             nc.vector.quantize_mx(
                 out=codes[:].bitcast(FP8X4), scales=out_plane[:, cols], in_=rounded[:].rearrange("p j r -> p (j r)")
             )
             nc.sync.dma_start(out_words[:, cols], codes[:].bitcast(I32))
         for q in range(4):
-            nc.sync.dma_start(out_2[0, 4 * q : 4 * q + 4, :].bitcast(I32), out_plane[32 * q : 32 * q + 4, :].bitcast(I32))
+            queue = nc.sync if q % 2 == 0 else nc.scalar
+            queue.dma_start(out_2[0, 4 * q : 4 * q + 4, :].bitcast(I32), out_plane[32 * q : 32 * q + 4, :].bitcast(I32))

@@ -24,6 +24,9 @@ PASSES = K // (P * PACK)
 BLOCKS = S // P
 HALF = S // 2
 CHUNK = 2 * P
+CHUNKS = S // CHUNK
+SWAPPED = (2, 3, 7)
+CLEAR_SPLIT = 2560
 GAIN_ROW = P - 2
 SHIFT_ROW = P - 1
 
@@ -42,36 +45,38 @@ def tile_picked_zdq_linnone_po_kernel(
 
         offsets = keep.tile([P, S // 16], U16, name="offsets")
         nc.sync.dma_start(offsets[:], offs)
-
-        scale_table = keep.tile([P, T], U8, name="scale_table")
-        nc.vector.memset(scale_table[:].bitcast(I32), 0)
-        zero = keep.tile([P, 1], F32, name="zero", tag="words0", align_bytes=64)
-        nc.gpsimd.memset(zero[:], 0.0)
-        ident = keep.tile([P, P], F32, name="ident")
-        make_identity(nc, ident[:])
         row_table = keep.tile([P, T], F32, name="row_table")
-        nc.vector.memset(row_table[:GAIN_ROW, : T // 2], 0.0)
-        nc.scalar.copy(row_table[:GAIN_ROW, T // 2 :], zero[:GAIN_ROW, :].to_broadcast([GAIN_ROW, T // 2]))
         nc.sync.dma_start(row_table[GAIN_ROW : GAIN_ROW + 1, :], gain[0:1, :])
         nc.sync.dma_start(row_table[SHIFT_ROW : SHIFT_ROW + 1, :], shift[0:1, :])
         wsum_cols = keep.tile([P, PACK], F32, name="wsum_cols")
-        nc.sync.dma_start(wsum_cols[:], wsum.rearrange("(p t) o -> p (t o)", t=PACK))
+        nc.gpsimd.dma_start(wsum_cols[:], wsum.rearrange("(p t) o -> p (t o)", t=PACK))
+        scale_table = keep.tile([P, T], U8, name="scale_table")
+        nc.vector.memset(scale_table[:].bitcast(I32), 0)
+        zeros = []
+        for i in range(3):
+            zero = keep.tile([P, 1], F32, name="zero%d" % i, tag=("w_raw1", "words0", "zero")[i], align_bytes=64)
+            nc.gpsimd.memset(zero[:], 0.0)
+            zeros.append(zero)
+        ident = keep.tile([P, P], F32, name="ident")
+        make_identity(nc, ident[:])
+        for i in range(2):
+            nc.vector.tensor_copy(row_table[:GAIN_ROW, 64 * i : 64 * (i + 1)], zeros[i][:GAIN_ROW, :].to_broadcast([GAIN_ROW, 64]))
+        nc.vector.memset(row_table[:GAIN_ROW, P:CLEAR_SPLIT], 0.0)
+        nc.scalar.copy(row_table[:GAIN_ROW, CLEAR_SPLIT:], zeros[2][:GAIN_ROW, :].to_broadcast([GAIN_ROW, T - CLEAR_SPLIT]))
 
         w_raw = []
         for o in range(PASSES):
             raw = keep.tile([P, PACK, N], F32, name="w_raw%d" % o, tag=("words1", "w_raw1")[o], align_bytes=64)
             nc.sync.dma_start(raw[:], w1[512 * o : 512 * (o + 1), :].rearrange("(p r) m -> p r m", r=PACK))
             w_raw.append(raw)
-        for q in range(4):
-            queue = nc.sync if q % 2 == 0 else nc.gpsimd
-            queue.dma_start(
-                scale_table[32 * q : 32 * q + 8, :].bitcast(I32), x_scales[:, 4 * q : 4 * q + 4, :].bitcast(I32)
-            )
+            if o == 0:
+                for q in range(4):
+                    nc.sync.dma_start(
+                        scale_table[32 * q : 32 * q + 8, :].bitcast(I32), x_scales[:, 4 * q : 4 * q + 4, :].bitcast(I32)
+                    )
 
         picked_rows = keep.tile([P, S], F32, name="picked_rows")
         nc.vector.tensor_copy(picked_rows[:], row_table[:].indirect(offsets[:]))
-        x_planes = keep.tile([P, S], U8, name="x_planes", align_bytes=64)
-        nc.vector.tensor_copy(x_planes[:], scale_table[:].indirect(offsets[:]))
 
         w_codes, w_planes = [], []
         for o in range(PASSES):
@@ -91,89 +96,130 @@ def tile_picked_zdq_linnone_po_kernel(
             nc.sync.dma_start(table[:].bitcast(I32), x_words[o].rearrange("p c r -> p (c r)").bitcast(I32))
             word_table.append(table)
 
+        x_planes = keep.tile([P, S], U8, name="x_planes", align_bytes=64)
+        nc.vector.tensor_copy(x_planes[:], scale_table[:].indirect(offsets[:]))
+
         factors = keep.tile([P, BLOCKS, 2], F32, name="factors", tag="w_raw1", align_bytes=64)
         for g in range(BLOCKS // 4):
             bank = psum.tile([P, 4, P], F32, name="turned_rows", tag="bank%d" % g)
             for i in range(4):
                 b = 4 * g + i
                 nc.tensor.transpose(bank[:, i, :], picked_rows[:, P * b : P * (b + 1)], ident[:])
-            nc.scalar.copy(factors[:, 4 * g : 4 * g + 4, :], bank[:, :, GAIN_ROW:])
-        shift_rows = keep.tile([P, S], F32, name="shift_rows")
-        for g in range(BLOCKS // 4):
-            bank = psum.tile([P, 4, P], F32, name="spread_shift", tag="bank%d" % (2 + g))
-            for i in range(4):
-                nc.tensor.transpose(bank[:, i, :], factors[:, 4 * g + i, 1:2].to_broadcast([P, P]), ident[:])
-            nc.scalar.copy(shift_rows[:, HALF * g : HALF * (g + 1)], bank[:].rearrange("p i j -> p (i j)"))
-        sums = [psum.tile([P, N], F32, name="sums%d" % b, tag="bank%d" % b) for b in range(BLOCKS)]
+            nc.vector.tensor_copy(factors[:, 4 * g : 4 * g + 4, :], bank[:, :, GAIN_ROW:])
+        spread_wsum = psum.tile([P, PACK, P], F32, name="spread_wsum", tag="bank7")
+        for t in range(PACK):
+            nc.tensor.transpose(spread_wsum[:, t, :], wsum_cols[:, t : t + 1].to_broadcast([P, P]), ident[:])
+        offset_terms = {}
+        plain = [b for b in range(BLOCKS) if b not in SWAPPED]
+        for g in range(0, len(plain), 4):
+            group = plain[g : g + 4]
+            bank = psum.tile([P, len(group), P], F32, name="spread_shift", tag="bank%d" % (5 + g // 4))
+            for i, b in enumerate(group):
+                nc.tensor.transpose(bank[:, i, :], factors[:, b, 1:2].to_broadcast([P, P]), ident[:])
+            terms = keep.tile([P, len(group), PACK, P], F32, name="offset_terms%d" % g)
+            for t in range(PACK):
+                nc.scalar.activation(terms[:, :, t, :], bank[:], COPY, scale=wsum_cols[:, t : t + 1])
+            for i, b in enumerate(group):
+                offset_terms[b] = terms[:, i, :, :]
+        for b in SWAPPED:
+            term = keep.tile([P, PACK, P], F32, name="offset_term%d" % b)
+            nc.scalar.activation(term[:], spread_wsum[:], COPY, scale=factors[:, b, 1:2])
+            offset_terms[b] = term[:]
 
-        def gather_words(o, first, width):
-            codes = keep.tile([P, width], U32, name="x_codes%d_%d" % (o, first), align_bytes=64)
-            nc.vector.tensor_copy(codes[:], word_table[o][:].indirect(offsets[:, first // 16 : (first + width) // 16]))
-            return codes
+        sums = {}
+        picked = {}
 
-        def multiply(o, codes, first, width):
-            for c in range(0, width, P):
-                nc.tensor.matmul_mx(
-                    out=sums[(first + c) // P][:],
-                    lhsT=codes[:, c : c + P].bitcast(FP8X4),
-                    lhsT_scale=x_planes[4 * o :, first + c : first + c + P],
-                    rhs=w_codes[o][:].bitcast(FP8X4),
-                    rhs_scale=w_planes[o][:],
-                    start=(o == 0),
-                    stop=(o == PASSES - 1),
-                )
+        def gather(o, h):
+            codes = keep.tile([P, HALF], U32, name="x_codes%d_%d" % (o, h), align_bytes=64)
+            nc.vector.tensor_copy(codes[:], word_table[o][:].indirect(offsets[:, HALF * h // 16 : HALF * (h + 1) // 16]))
+            picked[o, h] = codes
+
+        def multiply(o, b):
+            if o == 0:
+                sums[b] = psum.tile([P, N], F32, name="sums%d" % b, tag="bank%d" % b)
+            h, i = divmod(b, BLOCKS // 2)
+            nc.tensor.matmul_mx(
+                out=sums[b][:],
+                lhsT=picked[o, h][:, P * i : P * (i + 1)].bitcast(FP8X4),
+                lhsT_scale=x_planes[4 * o :, P * b : P * (b + 1)],
+                rhs=w_codes[o][:].bitcast(FP8X4),
+                rhs_scale=w_planes[o][:],
+                start=(o == 0),
+                stop=(o == PASSES - 1),
+            )
 
         out_rows = out_0.rearrange("(p t) j -> p t j", t=PACK)
-        results = [keep.tile([P, PACK, CHUNK], F32, name="result%d" % c) for c in range(S // CHUNK)]
-
-        def finish(b):
-            scaled = keep.tile([P, PACK, P], F32, name="scaled%d" % b)
-            nc.scalar.activation(
-                scaled[:], sums[b][:].rearrange("j (p t) -> j t p", t=PACK), COPY, scale=factors[:, b, 0:1]
-            )
-            turned = psum.tile([P, PACK, P], F32, name="turned%d" % b, tag="bank%d" % b)
-            for t in range(PACK):
-                nc.tensor.transpose(turned[:, t, :], scaled[:, t, :], ident[:])
-            chunk, i = divmod(b, CHUNK // P)
-            nc.vector.tensor_tensor(
-                results[chunk][:, :, P * i : P * (i + 1)], turned[:], offset_terms[b // 4][:, :, P * (b % 4) : P * (b % 4 + 1)], ADD
-            )
-            if i == CHUNK // P - 1:
-                nc.sync.dma_start(out_rows[:, :, CHUNK * chunk : CHUNK * (chunk + 1)], results[chunk][:])
-
-        for h in range(2):
-            multiply(0, gather_words(0, HALF * h, HALF), HALF * h, HALF)
-        offset_terms = []
-        for h in range(2):
-            term = keep.tile([P, PACK, HALF], F32, name="term%d" % h, tag=("term0", "words0")[h], align_bytes=64)
-            rows = shift_rows[:, HALF * h : HALF * (h + 1)]
-            for t in range(PACK):
-                if h == 0:
-                    nc.scalar.activation(term[:, t, :], rows, COPY, scale=wsum_cols[:, t : t + 1])
-                else:
-                    nc.vector.tensor_scalar(term[:, t, :], rows, wsum_cols[:, t : t + 1], None, MULT)
-            offset_terms.append(term)
-        last = [gather_words(1, HALF * h, HALF) for h in range(2)]
-        multiply(1, last[0], 0, HALF)
-        for b in range(2):
-            finish(b)
-        multiply(1, last[1], HALF, HALF)
-        for b in range(2, BLOCKS):
-            finish(b)
-
         out_words = out_1[0].rearrange("p j r -> p (j r)").bitcast(I32)
         out_plane = keep.tile([P, S], U8, name="out_plane", align_bytes=64)
-        for h in range(2):
-            copy = (nc.scalar.copy, nc.vector.tensor_copy)[h]
-            rounded = keep.tile([P, HALF, PACK], BF16, name="rounded%d" % h, tag=("w_raw1", "rounded1")[h], align_bytes=64)
-            for c in range(2):
-                interleave(copy, rounded[:, CHUNK * c : CHUNK * (c + 1), :], results[2 * h + c][:])
-            codes = keep.tile([P, HALF], U32, name="out_codes%d" % h, align_bytes=64)
-            cols = slice(HALF * h, HALF * (h + 1))
+        results = [keep.tile([P, PACK, CHUNK], F32, name="result%d" % c) for c in range(CHUNKS)]
+        rounded = [keep.tile([P, CHUNK, PACK], BF16, name="rounded%d" % c, align_bytes=64) for c in range(CHUNKS)]
+        scaled = [keep.tile([P, PACK, P], F32, name="scaled%d" % b) for b in range(BLOCKS)]
+        turned = {}
+
+        def scale(b):
+            dealt = sums[b][:].rearrange("j (p t) -> j t p", t=PACK)
+            if b in SWAPPED:
+                nc.vector.scalar_tensor_tensor(scaled[b][:], dealt, factors[:, b, 0:1], offset_terms[b], MULT, ADD)
+            else:
+                nc.scalar.activation(scaled[b][:], dealt, COPY, scale=factors[:, b, 0:1])
+
+        def turn(b):
+            turned[b] = psum.tile([P, PACK, P], F32, name="turned%d" % b, tag="bank%d" % b)
+            for t in range(PACK):
+                nc.tensor.transpose(turned[b][:, t, :], scaled[b][:, t, :], ident[:])
+
+        def finish(b):
+            c, i = divmod(b, 2)
+            if b in SWAPPED:
+                nc.scalar.copy(results[c][:, :, P * i : P * (i + 1)], turned[b][:])
+            else:
+                nc.vector.tensor_tensor(results[c][:, :, P * i : P * (i + 1)], turned[b][:], offset_terms[b], ADD)
+            if i == 1:
+                nc.sync.dma_start(out_rows[:, :, CHUNK * c : CHUNK * (c + 1)], results[c][:])
+
+        def round_block(b):
+            c, i = divmod(b, 2)
+            if b in SWAPPED:
+                nc.scalar.copy(rounded[c][:, P * i : P * (i + 1), :], turned[b][:].rearrange("p t j -> p j t"))
+            else:
+                interleave(nc.vector.tensor_copy, rounded[c][:, P * i : P * (i + 1), :], results[c][:, :, P * i : P * (i + 1)])
+
+        def quantise(c):
+            codes = keep.tile([P, CHUNK], U32, name="out_codes%d" % c, align_bytes=64)
+            cols = slice(CHUNK * c, CHUNK * (c + 1))
             nc.vector.quantize_mx(
-                out=codes[:].bitcast(FP8X4), scales=out_plane[:, cols], in_=rounded[:].rearrange("p j r -> p (j r)")
+                out=codes[:].bitcast(FP8X4), scales=out_plane[:, cols], in_=rounded[c][:].rearrange("p j r -> p (j r)")
             )
             nc.sync.dma_start(out_words[:, cols], codes[:].bitcast(I32))
+
+        for h in range(2):
+            gather(0, h)
+        for b in range(BLOCKS):
+            multiply(0, b)
+        for h in range(2):
+            gather(1, h)
+        for b in range(4):
+            multiply(1, b)
+            scale(b)
+        for b in (0, 1):
+            turn(b)
+            finish(b)
+        for b in (4, 5):
+            multiply(1, b)
+            scale(b)
+        for b in (2, 3):
+            turn(b)
+            finish(b)
+        for b in (6, 7):
+            multiply(1, b)
+            scale(b)
+        for b in range(4, BLOCKS):
+            turn(b)
+            finish(b)
+        for c in range(CHUNKS):
+            round_block(2 * c)
+            round_block(2 * c + 1)
+            quantise(c)
         for q in range(4):
             queue = nc.sync if q % 2 == 0 else nc.scalar
             queue.dma_start(out_2[0, 4 * q : 4 * q + 4, :].bitcast(I32), out_plane[32 * q : 32 * q + 4, :].bitcast(I32))

@@ -26,7 +26,7 @@ HALF = S // 2
 CHUNK = 2 * P
 CHUNKS = S // CHUNK
 SWAPPED = (2, 3, 7)
-CLEAR_SPLIT = 2560
+CLEAR_SPLIT = 2048
 GAIN_ROW = P - 2
 SHIFT_ROW = P - 1
 
@@ -45,35 +45,48 @@ def tile_picked_zdq_linnone_po_kernel(
 
         offsets = keep.tile([P, S // 16], U16, name="offsets")
         nc.sync.dma_start(offsets[:], offs)
-        row_table = keep.tile([P, T], F32, name="row_table")
+        scale_table = keep.tile([P, T], U8, name="scale_table", tag="words1", align_bytes=64)
+        nc.sync.dma_start(scale_table[:32, :].bitcast(I32), x_scales.rearrange("o q c -> (o q) c").bitcast(I32))
+        row_table = keep.tile([P, T], F32, name="row_table", align_bytes=64)
         nc.sync.dma_start(row_table[GAIN_ROW : GAIN_ROW + 1, :], gain[0:1, :])
         nc.sync.dma_start(row_table[SHIFT_ROW : SHIFT_ROW + 1, :], shift[0:1, :])
+        nc.vector.memset(scale_table[32:64, :].bitcast(I32), 0)
+        nc.vector.memset(scale_table[64:, :].bitcast(I32), 0)
         wsum_cols = keep.tile([P, PACK], F32, name="wsum_cols")
-        nc.gpsimd.dma_start(wsum_cols[:], wsum.rearrange("(p t) o -> p (t o)", t=PACK))
-        scale_table = keep.tile([P, T], U8, name="scale_table")
-        nc.vector.memset(scale_table[:].bitcast(I32), 0)
-        zeros = []
-        for i in range(3):
-            zero = keep.tile([P, 1], F32, name="zero%d" % i, tag=("w_raw1", "words0", "zero")[i], align_bytes=64)
-            nc.gpsimd.memset(zero[:], 0.0)
-            zeros.append(zero)
-        ident = keep.tile([P, P], F32, name="ident")
-        make_identity(nc, ident[:])
-        for i in range(2):
-            nc.vector.tensor_copy(row_table[:GAIN_ROW, 64 * i : 64 * (i + 1)], zeros[i][:GAIN_ROW, :].to_broadcast([GAIN_ROW, 64]))
-        nc.vector.memset(row_table[:GAIN_ROW, P:CLEAR_SPLIT], 0.0)
-        nc.scalar.copy(row_table[:GAIN_ROW, CLEAR_SPLIT:], zeros[2][:GAIN_ROW, :].to_broadcast([GAIN_ROW, T - CLEAR_SPLIT]))
-
+        nc.sync.dma_start(wsum_cols[:], wsum.rearrange("(p t) o -> p (t o)", t=PACK))
         w_raw = []
         for o in range(PASSES):
-            raw = keep.tile([P, PACK, N], F32, name="w_raw%d" % o, tag=("words1", "w_raw1")[o], align_bytes=64)
+            raw = keep.tile([P, PACK, N], F32, name="w_raw%d" % o, align_bytes=64)
             nc.sync.dma_start(raw[:], w1[512 * o : 512 * (o + 1), :].rearrange("(p r) m -> p r m", r=PACK))
             w_raw.append(raw)
+
+        zero = keep.tile([P, 1], F32, name="zero")
+        nc.gpsimd.memset(zero[:], 0.0)
+        ident = keep.tile([P, P], F32, name="ident")
+        make_identity(nc, ident[:])
+        nc.vector.memset(row_table[:GAIN_ROW, :CLEAR_SPLIT], 0.0)
+        nc.scalar.copy(row_table[:GAIN_ROW, CLEAR_SPLIT:], zero[:GAIN_ROW, :].to_broadcast([GAIN_ROW, T - CLEAR_SPLIT]))
+
+        picked_scales = keep.tile([P, S], U8, name="picked_scales")
+        nc.vector.tensor_copy(picked_scales[:], scale_table[:].indirect(offsets[:]))
+        word_table, x_planes = [], []
+
+        def place_scales(o):
+            plane = keep.tile([P, S], U8, name="x_plane%d" % o, tag=("x_plane0", "w_grouped0")[o], align_bytes=64)
+            nc.gpsimd.memset(plane[:].bitcast(I32), 0)
+            x_planes.append(plane)
+            for q in range(4):
+                row = 16 * o + 4 * q
+                nc.sync.dma_start(
+                    plane[32 * q + 4 * o : 32 * q + 4 * o + 4, :].bitcast(I32), picked_scales[row : row + 4, :].bitcast(I32)
+                )
+
+        for o in range(PASSES):
+            table = keep.tile([P, T], U32, name="word_table%d" % o, tag="words%d" % o, align_bytes=64)
+            nc.sync.dma_start(table[:].bitcast(I32), x_words[o].rearrange("p c r -> p (c r)").bitcast(I32))
+            word_table.append(table)
             if o == 0:
-                for q in range(4):
-                    nc.sync.dma_start(
-                        scale_table[32 * q : 32 * q + 8, :].bitcast(I32), x_scales[:, 4 * q : 4 * q + 4, :].bitcast(I32)
-                    )
+                place_scales(0)
 
         picked_rows = keep.tile([P, S], F32, name="picked_rows")
         nc.vector.tensor_copy(picked_rows[:], row_table[:].indirect(offsets[:]))
@@ -82,7 +95,7 @@ def tile_picked_zdq_linnone_po_kernel(
         for o in range(PASSES):
             grouped = keep.tile([P, N, PACK], BF16, name="w_grouped%d" % o, align_bytes=64)
             interleave(nc.scalar.copy, grouped[:], w_raw[o][:])
-            codes = keep.tile([P, N], U32, name="w_codes%d" % o, align_bytes=64)
+            codes = keep.tile([P, N], U32, name="w_codes%d" % o, tag=("w_codes0", "row_table")[o], align_bytes=64)
             plane = keep.tile([P, N], U8, name="w_plane%d" % o, align_bytes=64)
             nc.vector.quantize_mx(
                 out=codes[:].bitcast(FP8X4), scales=plane[:], in_=grouped[:].rearrange("p m r -> p (m r)")
@@ -90,15 +103,7 @@ def tile_picked_zdq_linnone_po_kernel(
             w_codes.append(codes)
             w_planes.append(plane)
 
-        word_table = []
-        for o in range(PASSES):
-            table = keep.tile([P, T], U32, name="word_table%d" % o, tag="words%d" % o, align_bytes=64)
-            nc.sync.dma_start(table[:].bitcast(I32), x_words[o].rearrange("p c r -> p (c r)").bitcast(I32))
-            word_table.append(table)
-
-        x_planes = keep.tile([P, S], U8, name="x_planes", align_bytes=64)
-        nc.vector.tensor_copy(x_planes[:], scale_table[:].indirect(offsets[:]))
-
+        place_scales(1)
         factors = keep.tile([P, BLOCKS, 2], F32, name="factors", tag="w_raw1", align_bytes=64)
         for g in range(BLOCKS // 4):
             bank = psum.tile([P, 4, P], F32, name="turned_rows", tag="bank%d" % g)
@@ -141,7 +146,7 @@ def tile_picked_zdq_linnone_po_kernel(
             nc.tensor.matmul_mx(
                 out=sums[b][:],
                 lhsT=picked[o, h][:, P * i : P * (i + 1)].bitcast(FP8X4),
-                lhsT_scale=x_planes[4 * o :, P * b : P * (b + 1)],
+                lhsT_scale=x_planes[o][4 * o :, P * b : P * (b + 1)],
                 rhs=w_codes[o][:].bitcast(FP8X4),
                 rhs_scale=w_planes[o][:],
                 start=(o == 0),

@@ -25,7 +25,9 @@ BLOCKS = S // P
 HALF = S // 2
 CHUNK = 2 * P
 CHUNKS = S // CHUNK
-SWAPPED = (2, 3, 7)
+SWAPPED = (2, 7)
+SCALAR_ROUNDS = (3,)
+ADDED = (6,)
 CLEAR_SPLIT = 2048
 GAIN_ROW = P - 2
 SHIFT_ROW = P - 1
@@ -73,13 +75,10 @@ def tile_picked_zdq_linnone_po_kernel(
 
         def place_scales(o):
             plane = keep.tile([P, S], U8, name="x_plane%d" % o, tag=("x_plane0", "w_grouped0")[o], align_bytes=64)
-            nc.gpsimd.memset(plane[:].bitcast(I32), 0)
+            (nc.gpsimd, nc.vector)[o].memset(plane[:].bitcast(I32), 0)
             x_planes.append(plane)
-            for q in range(4):
-                row = 16 * o + 4 * q
-                nc.sync.dma_start(
-                    plane[32 * q + 4 * o : 32 * q + 4 * o + 4, :].bitcast(I32), picked_scales[row : row + 4, :].bitcast(I32)
-                )
+            for i in range(4):
+                nc.sync.dma_start(plane[4 * o + i :: 32, :].bitcast(I32), picked_scales[16 * o + i : 16 * (o + 1) : 4, :].bitcast(I32))
 
         for o in range(PASSES):
             table = keep.tile([P, T], U32, name="word_table%d" % o, tag="words%d" % o, align_bytes=64)
@@ -111,26 +110,35 @@ def tile_picked_zdq_linnone_po_kernel(
                 b = 4 * g + i
                 nc.tensor.transpose(bank[:, i, :], picked_rows[:, P * b : P * (b + 1)], ident[:])
             nc.vector.tensor_copy(factors[:, 4 * g : 4 * g + 4, :], bank[:, :, GAIN_ROW:])
-        spread_wsum = psum.tile([P, PACK, P], F32, name="spread_wsum", tag="bank7")
+        spread = []
+        groups = [[b for b in range(4 * h, 4 * h + 4) if b not in SWAPPED + ADDED] for h in range(2)]
+        for h in range(2):
+            bank = psum.tile([P, len(groups[h]), P], F32, name="spread_shift", tag="bank%d" % (6 + h))
+            for i, b in enumerate(groups[h]):
+                nc.tensor.transpose(bank[:, i, :], factors[:, b, 1:2].to_broadcast([P, P]), ident[:])
+            spread.append(bank)
+        late_shift = keep.tile([P, len(groups[1]), P], F32, name="late_shift")
+        nc.scalar.copy(late_shift[:], spread[1][:])
+        spread_wsum = psum.tile([P, PACK, P], F32, name="spread_wsum", tag="bank5")
         for t in range(PACK):
             nc.tensor.transpose(spread_wsum[:, t, :], wsum_cols[:, t : t + 1].to_broadcast([P, P]), ident[:])
         offset_terms = {}
-        plain = [b for b in range(BLOCKS) if b not in SWAPPED]
-        for g in range(0, len(plain), 4):
-            group = plain[g : g + 4]
-            bank = psum.tile([P, len(group), P], F32, name="spread_shift", tag="bank%d" % (5 + g // 4))
-            for i, b in enumerate(group):
-                nc.tensor.transpose(bank[:, i, :], factors[:, b, 1:2].to_broadcast([P, P]), ident[:])
-            terms = keep.tile([P, len(group), PACK, P], F32, name="offset_terms%d" % g)
-            for t in range(PACK):
-                nc.scalar.activation(terms[:, :, t, :], bank[:], COPY, scale=wsum_cols[:, t : t + 1])
-            for i, b in enumerate(group):
-                offset_terms[b] = terms[:, i, :, :]
-        for b in SWAPPED:
-            term = keep.tile([P, PACK, P], F32, name="offset_term%d" % b)
+        for b in SWAPPED + ADDED:
+            term = keep.tile([P, PACK, P], F32, name="swapped_term%d" % b)
             nc.scalar.activation(term[:], spread_wsum[:], COPY, scale=factors[:, b, 1:2])
             offset_terms[b] = term[:]
 
+        def make_terms(h):
+            terms = keep.tile([P, len(groups[h]), PACK, P], F32, name="offset_terms%d" % h, tag=("terms0", "words0")[h], align_bytes=64)
+            for t in range(PACK):
+                if h == 0:
+                    nc.scalar.activation(terms[:, :, t, :], spread[0][:], COPY, scale=wsum_cols[:, t : t + 1])
+                else:
+                    nc.vector.tensor_scalar(terms[:, :, t, :], late_shift[:], wsum_cols[:, t : t + 1], None, MULT)
+            for i, b in enumerate(groups[h]):
+                offset_terms[b] = terms[:, i, :, :]
+
+        make_terms(0)
         sums = {}
         picked = {}
 
@@ -157,9 +165,10 @@ def tile_picked_zdq_linnone_po_kernel(
         out_words = out_1[0].rearrange("p j r -> p (j r)").bitcast(I32)
         out_plane = keep.tile([P, S], U8, name="out_plane", align_bytes=64)
         results = [keep.tile([P, PACK, CHUNK], F32, name="result%d" % c) for c in range(CHUNKS)]
-        rounded = [keep.tile([P, CHUNK, PACK], BF16, name="rounded%d" % c, align_bytes=64) for c in range(CHUNKS)]
-        scaled = [keep.tile([P, PACK, P], F32, name="scaled%d" % b) for b in range(BLOCKS)]
-        turned = {}
+        rounded = {}
+        scaled = [keep.tile([P, PACK, P], F32, name="scaled%d" % b, align_bytes=64) for b in range(BLOCKS)]
+
+        turned_banks = {}
 
         def scale(b):
             dealt = sums[b][:].rearrange("j (p t) -> j t p", t=PACK)
@@ -168,29 +177,27 @@ def tile_picked_zdq_linnone_po_kernel(
             else:
                 nc.scalar.activation(scaled[b][:], dealt, COPY, scale=factors[:, b, 0:1])
 
-        def turn(b):
-            turned[b] = psum.tile([P, PACK, P], F32, name="turned%d" % b, tag="bank%d" % b)
-            for t in range(PACK):
-                nc.tensor.transpose(turned[b][:, t, :], scaled[b][:, t, :], ident[:])
-
         def finish(b):
+            turned = turned_banks[b] = psum.tile([P, PACK, P], F32, name="turned%d" % b, tag="bank%d" % b)
+            for t in range(PACK):
+                if b in ADDED:
+                    nc.tensor.matmul(turned[:, t, :], offset_terms[b][:, t, :], ident[:], start=True, stop=False, is_transpose=True)
+                    nc.tensor.matmul(turned[:, t, :], scaled[b][:, t, :], ident[:], start=False, stop=True, is_transpose=True)
+                else:
+                    nc.tensor.transpose(turned[:, t, :], scaled[b][:, t, :], ident[:])
             c, i = divmod(b, 2)
-            if b in SWAPPED:
-                nc.scalar.copy(results[c][:, :, P * i : P * (i + 1)], turned[b][:])
+            if b in SWAPPED + ADDED:
+                nc.scalar.copy(results[c][:, :, P * i : P * (i + 1)], turned[:])
             else:
-                nc.vector.tensor_tensor(results[c][:, :, P * i : P * (i + 1)], turned[b][:], offset_terms[b], ADD)
-            if i == 1:
+                nc.vector.tensor_tensor(results[c][:, :, P * i : P * (i + 1)], turned[:], offset_terms[b], ADD)
+            if c == 0:
+                nc.sync.dma_start(out_rows[:, :, P * b : P * (b + 1)], results[c][:, :, P * i : P * (i + 1)])
+            elif i == 1:
                 nc.sync.dma_start(out_rows[:, :, CHUNK * c : CHUNK * (c + 1)], results[c][:])
 
-        def round_block(b):
-            c, i = divmod(b, 2)
-            if b in SWAPPED:
-                nc.scalar.copy(rounded[c][:, P * i : P * (i + 1), :], turned[b][:].rearrange("p t j -> p j t"))
-            else:
-                interleave(nc.vector.tensor_copy, rounded[c][:, P * i : P * (i + 1), :], results[c][:, :, P * i : P * (i + 1)])
-
         def quantise(c):
-            codes = keep.tile([P, CHUNK], U32, name="out_codes%d" % c, align_bytes=64)
+            tag = ("scaled5", "scaled7", "out_codes2", "out_codes3")[c]
+            codes = keep.tile([P, CHUNK], U32, name="out_codes%d" % c, tag=tag, align_bytes=64)
             cols = slice(CHUNK * c, CHUNK * (c + 1))
             nc.vector.quantize_mx(
                 out=codes[:].bitcast(FP8X4), scales=out_plane[:, cols], in_=rounded[c][:].rearrange("p j r -> p (j r)")
@@ -199,6 +206,7 @@ def tile_picked_zdq_linnone_po_kernel(
 
         for h in range(2):
             gather(0, h)
+        make_terms(1)
         for b in range(BLOCKS):
             multiply(0, b)
         for h in range(2):
@@ -206,24 +214,30 @@ def tile_picked_zdq_linnone_po_kernel(
         for b in range(4):
             multiply(1, b)
             scale(b)
-        for b in (0, 1):
-            turn(b)
-            finish(b)
-        for b in (4, 5):
-            multiply(1, b)
-            scale(b)
-        for b in (2, 3):
-            turn(b)
-            finish(b)
-        for b in (6, 7):
-            multiply(1, b)
-            scale(b)
-        for b in range(4, BLOCKS):
-            turn(b)
-            finish(b)
         for c in range(CHUNKS):
-            round_block(2 * c)
-            round_block(2 * c + 1)
+            finish(2 * c)
+            finish(2 * c + 1)
+            if c < 2:
+                for b in (2 * c + 4, 2 * c + 5):
+                    multiply(1, b)
+                    scale(b)
+        for c in range(CHUNKS):
+            tag = ("rounded0", "x_codes1_1", "rounded2", "rounded3")[c]
+            rounded[c] = keep.tile([P, CHUNK, PACK], BF16, name="rounded%d" % c, tag=tag, align_bytes=64)
+            for i in range(2):
+                b = 2 * c + i
+                if c == 0 or b == 3:
+                    if b != 1:
+                        cols = slice(P * i, CHUNK)
+                        nc.gpsimd.tensor_scalar(
+                            rounded[c][:, cols, :], results[c][:, :, cols].rearrange("p t j -> p j t"), 1.0, -0.0, MULT, ADD
+                        )
+                elif b in SWAPPED:
+                    nc.scalar.copy(rounded[c][:, P * i : P * (i + 1), :], turned_banks[b][:].rearrange("p t j -> p j t"))
+                else:
+                    copy = nc.scalar.copy if b in SCALAR_ROUNDS else nc.vector.tensor_copy
+                    interleave(copy, rounded[c][:, P * i : P * (i + 1), :], results[c][:, :, P * i : P * (i + 1)])
+        for c in range(CHUNKS):
             quantise(c)
         for q in range(4):
             queue = nc.sync if q % 2 == 0 else nc.scalar

@@ -28,9 +28,14 @@ CHUNKS = S // CHUNK
 SWAPPED = (2, 7)
 SCALAR_ROUNDS = (3,)
 ADDED = (6,)
-CLEAR_SPLIT = 2048
-GAIN_ROW = P - 2
+SCALAR_CLEARS = 2048
+VECTOR_CLEARS = 2560
+FIRST_CLEARED = 7
+GAIN_ROW = P // 2 - 1
 SHIFT_ROW = P - 1
+TABLE = 4 * T
+WORDS0 = TABLE + 16 * N
+SCALES = WORDS0 + TABLE + 2 * S
 
 
 def interleave(copy, dst, src):
@@ -43,31 +48,42 @@ def tile_picked_zdq_linnone_po_kernel(
     nc = tc.nc
     with ExitStack() as ctx:
         keep = ctx.enter_context(tc.tile_pool(name="keep", bufs=1))
+        reuse = ctx.enter_context(tc.tile_pool(name="reuse", bufs=1))
         psum = ctx.enter_context(tc.psum_pool(name="psum", bufs=1))
 
-        offsets = keep.tile([P, S // 16], U16, name="offsets")
-        nc.sync.dma_start(offsets[:], offs)
-        scale_table = keep.tile([P, T], U8, name="scale_table", tag="words1", align_bytes=64)
-        nc.sync.dma_start(scale_table[:32, :].bitcast(I32), x_scales.rearrange("o q c -> (o q) c").bitcast(I32))
-        row_table = keep.tile([P, T], F32, name="row_table", align_bytes=64)
+        def placed(shape, dtype, name, offset):
+            return reuse.tile(shape, dtype, name=name, align_bytes=64, offset=offset)
+
+        row_table = placed([P, T], F32, "row_table", 0)
         nc.sync.dma_start(row_table[GAIN_ROW : GAIN_ROW + 1, :], gain[0:1, :])
         nc.sync.dma_start(row_table[SHIFT_ROW : SHIFT_ROW + 1, :], shift[0:1, :])
-        nc.vector.memset(scale_table[32:64, :].bitcast(I32), 0)
-        nc.vector.memset(scale_table[64:, :].bitcast(I32), 0)
+        offsets = keep.tile([P, S // 16], U16, name="offsets")
+        nc.sync.dma_start(offsets[:], offs)
         wsum_cols = keep.tile([P, PACK], F32, name="wsum_cols")
         nc.sync.dma_start(wsum_cols[:], wsum.rearrange("(p t) o -> p (t o)", t=PACK))
-        w_raw = []
-        for o in range(PASSES):
-            raw = keep.tile([P, PACK, N], F32, name="w_raw%d" % o, align_bytes=64)
-            nc.sync.dma_start(raw[:], w1[512 * o : 512 * (o + 1), :].rearrange("(p r) m -> p r m", r=PACK))
-            w_raw.append(raw)
+        w_rows = w1.rearrange("(o p r) m -> o p r m", o=PASSES, r=PACK)
+        w_raw = [keep.tile([P, PACK, N], F32, name="w_raw0", align_bytes=64)]
+        nc.sync.dma_start(w_raw[0][:], w_rows[0])
 
         zero = keep.tile([P, 1], F32, name="zero")
         nc.gpsimd.memset(zero[:], 0.0)
+        first_zero = placed([P, 32], F32, "first_zero", WORDS0 - 64)
+        nc.gpsimd.memset(first_zero[:], 0.0)
+        scale_table = placed([P, T], U8, "scale_table", SCALES)
+        scale_words = scale_table[:].bitcast(I32)
+        nc.vector.memset(scale_words[:, 1:], 0)
+        nc.vector.memset(scale_words[:, :1], 0)
+        nc.sync.dma_start(scale_table[::4, :].bitcast(I32), x_scales.rearrange("o q c -> (o q) c").bitcast(I32))
+        upper = slice(GAIN_ROW + 1, SHIFT_ROW)
+        nc.vector.tensor_copy(row_table[:GAIN_ROW, :FIRST_CLEARED], first_zero[:GAIN_ROW, :FIRST_CLEARED])
+        nc.vector.memset(row_table[:GAIN_ROW, FIRST_CLEARED:VECTOR_CLEARS], 0.0)
+        w_raw.append(placed([P, PACK, N], F32, "w_raw1", TABLE))
+        nc.sync.dma_start(w_raw[1][:], w_rows[1])
+        nc.scalar.copy(row_table[upper, :SCALAR_CLEARS], zero[upper, :].to_broadcast([GAIN_ROW, SCALAR_CLEARS]))
+        nc.gpsimd.memset(row_table[upper, SCALAR_CLEARS:], 0.0)
+        nc.gpsimd.memset(row_table[:GAIN_ROW, VECTOR_CLEARS:], 0.0)
         ident = keep.tile([P, P], F32, name="ident")
         make_identity(nc, ident[:])
-        nc.vector.memset(row_table[:GAIN_ROW, :CLEAR_SPLIT], 0.0)
-        nc.scalar.copy(row_table[:GAIN_ROW, CLEAR_SPLIT:], zero[:GAIN_ROW, :].to_broadcast([GAIN_ROW, T - CLEAR_SPLIT]))
 
         picked_scales = keep.tile([P, S], U8, name="picked_scales")
         nc.vector.tensor_copy(picked_scales[:], scale_table[:].indirect(offsets[:]))
@@ -78,23 +94,23 @@ def tile_picked_zdq_linnone_po_kernel(
             (nc.gpsimd, nc.vector)[o].memset(plane[:].bitcast(I32), 0)
             x_planes.append(plane)
             for i in range(4):
-                nc.sync.dma_start(plane[4 * o + i :: 32, :].bitcast(I32), picked_scales[16 * o + i : 16 * (o + 1) : 4, :].bitcast(I32))
+                nc.sync.dma_start(plane[4 * o + i :: 32, :].bitcast(I32), picked_scales[64 * o + 4 * i : 64 * (o + 1) : 16, :].bitcast(I32))
 
         for o in range(PASSES):
-            table = keep.tile([P, T], U32, name="word_table%d" % o, tag="words%d" % o, align_bytes=64)
+            table = placed([P, T], U32, "word_table%d" % o, (WORDS0, SCALES + 2 * S)[o])
             nc.sync.dma_start(table[:].bitcast(I32), x_words[o].rearrange("p c r -> p (c r)").bitcast(I32))
             word_table.append(table)
             if o == 0:
                 place_scales(0)
 
-        picked_rows = keep.tile([P, S], F32, name="picked_rows")
+        picked_rows = placed([P, S], F32, "picked_rows", SCALES - 2 * S)
         nc.vector.tensor_copy(picked_rows[:], row_table[:].indirect(offsets[:]))
 
         w_codes, w_planes = [], []
         for o in range(PASSES):
             grouped = keep.tile([P, N, PACK], BF16, name="w_grouped%d" % o, align_bytes=64)
             interleave(nc.scalar.copy, grouped[:], w_raw[o][:])
-            codes = keep.tile([P, N], U32, name="w_codes%d" % o, tag=("w_codes0", "row_table")[o], align_bytes=64)
+            codes = placed([P, N], U32, "w_codes%d" % o, (4 * N, 0)[o])
             plane = keep.tile([P, N], U8, name="w_plane%d" % o, align_bytes=64)
             nc.vector.quantize_mx(
                 out=codes[:].bitcast(FP8X4), scales=plane[:], in_=grouped[:].rearrange("p m r -> p (m r)")
@@ -103,13 +119,13 @@ def tile_picked_zdq_linnone_po_kernel(
             w_planes.append(plane)
 
         place_scales(1)
-        factors = keep.tile([P, BLOCKS, 2], F32, name="factors", tag="w_raw1", align_bytes=64)
+        factors = placed([P, BLOCKS, 2], F32, "factors", TABLE)
         for g in range(BLOCKS // 4):
             bank = psum.tile([P, 4, P], F32, name="turned_rows", tag="bank%d" % g)
             for i in range(4):
                 b = 4 * g + i
                 nc.tensor.transpose(bank[:, i, :], picked_rows[:, P * b : P * (b + 1)], ident[:])
-            nc.vector.tensor_copy(factors[:, 4 * g : 4 * g + 4, :], bank[:, :, GAIN_ROW:])
+            nc.vector.tensor_copy(factors[:, 4 * g : 4 * g + 4, :], bank[:, :, GAIN_ROW :: P // 2])
         spread = []
         groups = [[b for b in range(4 * h, 4 * h + 4) if b not in SWAPPED + ADDED] for h in range(2)]
         for h in range(2):
@@ -129,7 +145,7 @@ def tile_picked_zdq_linnone_po_kernel(
             offset_terms[b] = term[:]
 
         def make_terms(h):
-            terms = keep.tile([P, len(groups[h]), PACK, P], F32, name="offset_terms%d" % h, tag=("terms0", "words0")[h], align_bytes=64)
+            terms = placed([P, len(groups[h]), PACK, P], F32, "offset_terms%d" % h, (SCALES + 2 * S + TABLE, WORDS0)[h])
             for t in range(PACK):
                 if h == 0:
                     nc.scalar.activation(terms[:, :, t, :], spread[0][:], COPY, scale=wsum_cols[:, t : t + 1])

@@ -140,7 +140,7 @@ def tile_picked_zdq_linnone_po_kernel(
             nc.tensor.transpose(spread_wsum[:, t, :], wsum_cols[:, t : t + 1].to_broadcast([P, P]), ident[:])
         offset_terms = {}
         for b in SWAPPED + ADDED:
-            term = keep.tile([P, PACK, P], F32, name="swapped_term%d" % b)
+            term = keep.tile([P, PACK, P], F32, name="swapped_term%d" % b, align_bytes=64)
             nc.scalar.activation(term[:], spread_wsum[:], COPY, scale=factors[:, b, 1:2])
             offset_terms[b] = term[:]
 
@@ -238,16 +238,15 @@ def tile_picked_zdq_linnone_po_kernel(
                     multiply(1, b)
                     scale(b)
         for c in range(CHUNKS):
-            tag = ("rounded0", "x_codes1_1", "rounded2", "rounded3")[c]
+            tag = ("rounded0", "swapped_term7", "rounded2", "rounded3")[c]
             rounded[c] = keep.tile([P, CHUNK, PACK], BF16, name="rounded%d" % c, tag=tag, align_bytes=64)
             for i in range(2):
                 b = 2 * c + i
                 if c == 0 or b == 3:
-                    if b != 1:
-                        cols = slice(P * i, CHUNK)
-                        nc.gpsimd.tensor_scalar(
-                            rounded[c][:, cols, :], results[c][:, :, cols].rearrange("p t j -> p j t"), 1.0, -0.0, MULT, ADD
-                        )
+                    cols = slice(P * i, P * (i + 1))
+                    nc.gpsimd.tensor_scalar(
+                        rounded[c][:, cols, :], results[c][:, :, cols].rearrange("p t j -> p j t"), 1.0, -0.0, MULT, ADD
+                    )
                 elif b in SWAPPED:
                     nc.scalar.copy(rounded[c][:, P * i : P * (i + 1), :], turned_banks[b][:].rearrange("p t j -> p j t"))
                 else:

@@ -25,17 +25,22 @@ BLOCKS = S // P
 HALF = S // 2
 CHUNK = 2 * P
 CHUNKS = S // CHUNK
+
 SWAPPED = (2, 7)
-SCALAR_ROUNDS = (3,)
 ADDED = (6,)
-SCALAR_CLEARS = 2048
-VECTOR_CLEARS = 2560
-FIRST_CLEARED = 7
+GPSIMD_ROUNDS = (0, 1, 3)
+
 GAIN_ROW = P // 2 - 1
 SHIFT_ROW = P - 1
+SCALAR_CLEARS = 2048
+VECTOR_CLEARS = 2560
+FIRST_CLEARED = 31
+
 TABLE = 4 * T
 WORDS0 = TABLE + 16 * N
 SCALES = WORDS0 + TABLE + 2 * S
+WORDS1 = SCALES + 2 * S
+EARLY_TERMS = WORDS1 + TABLE
 
 
 def interleave(copy, dst, src):
@@ -66,16 +71,16 @@ def tile_picked_zdq_linnone_po_kernel(
         nc.sync.dma_start(w_raw[0][:], w_rows[0])
 
         zero = keep.tile([P, 1], F32, name="zero")
-        nc.gpsimd.memset(zero[:], 0.0)
-        first_zero = placed([P, 32], F32, "first_zero", WORDS0 - 64)
-        nc.gpsimd.memset(first_zero[:], 0.0)
+        upper = slice(GAIN_ROW + 1, SHIFT_ROW)
+        nc.gpsimd.memset(zero[upper, :], 0.0)
+        first_zero = placed([P, FIRST_CLEARED], F32, "first_zero", WORDS0 - 64)
+        nc.gpsimd.memset(first_zero[:GAIN_ROW, :], 0.0)
         scale_table = placed([P, T], U8, "scale_table", SCALES)
         scale_words = scale_table[:].bitcast(I32)
         nc.vector.memset(scale_words[:, 1:], 0)
         nc.vector.memset(scale_words[:, :1], 0)
         nc.sync.dma_start(scale_table[::4, :].bitcast(I32), x_scales.rearrange("o q c -> (o q) c").bitcast(I32))
-        upper = slice(GAIN_ROW + 1, SHIFT_ROW)
-        nc.vector.tensor_copy(row_table[:GAIN_ROW, :FIRST_CLEARED], first_zero[:GAIN_ROW, :FIRST_CLEARED])
+        nc.vector.tensor_copy(row_table[:GAIN_ROW, :FIRST_CLEARED], first_zero[:GAIN_ROW, :])
         nc.vector.memset(row_table[:GAIN_ROW, FIRST_CLEARED:VECTOR_CLEARS], 0.0)
         w_raw.append(placed([P, PACK, N], F32, "w_raw1", TABLE))
         nc.sync.dma_start(w_raw[1][:], w_rows[1])
@@ -94,10 +99,13 @@ def tile_picked_zdq_linnone_po_kernel(
             (nc.gpsimd, nc.vector)[o].memset(plane[:].bitcast(I32), 0)
             x_planes.append(plane)
             for i in range(4):
-                nc.sync.dma_start(plane[4 * o + i :: 32, :].bitcast(I32), picked_scales[64 * o + 4 * i : 64 * (o + 1) : 16, :].bitcast(I32))
+                nc.sync.dma_start(
+                    plane[4 * o + i :: 32, :].bitcast(I32),
+                    picked_scales[64 * o + 4 * i : 64 * (o + 1) : 16, :].bitcast(I32),
+                )
 
         for o in range(PASSES):
-            table = placed([P, T], U32, "word_table%d" % o, (WORDS0, SCALES + 2 * S)[o])
+            table = placed([P, T], U32, "word_table%d" % o, (WORDS0, WORDS1)[o])
             nc.sync.dma_start(table[:].bitcast(I32), x_words[o].rearrange("p c r -> p (c r)").bitcast(I32))
             word_table.append(table)
             if o == 0:
@@ -117,8 +125,8 @@ def tile_picked_zdq_linnone_po_kernel(
             )
             w_codes.append(codes)
             w_planes.append(plane)
-
         place_scales(1)
+
         factors = placed([P, BLOCKS, 2], F32, "factors", TABLE)
         for g in range(BLOCKS // 4):
             bank = psum.tile([P, 4, P], F32, name="turned_rows", tag="bank%d" % g)
@@ -126,37 +134,38 @@ def tile_picked_zdq_linnone_po_kernel(
                 b = 4 * g + i
                 nc.tensor.transpose(bank[:, i, :], picked_rows[:, P * b : P * (b + 1)], ident[:])
             nc.vector.tensor_copy(factors[:, 4 * g : 4 * g + 4, :], bank[:, :, GAIN_ROW :: P // 2])
-        spread = []
-        groups = [[b for b in range(4 * h, 4 * h + 4) if b not in SWAPPED + ADDED] for h in range(2)]
+
+        plain = [[b for b in range(4 * h, 4 * h + 4) if b not in SWAPPED + ADDED] for h in range(2)]
+        spread_shift = []
         for h in range(2):
-            bank = psum.tile([P, len(groups[h]), P], F32, name="spread_shift", tag="bank%d" % (6 + h))
-            for i, b in enumerate(groups[h]):
+            bank = psum.tile([P, len(plain[h]), P], F32, name="spread_shift", tag="bank%d" % (6 + h))
+            for i, b in enumerate(plain[h]):
                 nc.tensor.transpose(bank[:, i, :], factors[:, b, 1:2].to_broadcast([P, P]), ident[:])
-            spread.append(bank)
-        late_shift = keep.tile([P, len(groups[1]), P], F32, name="late_shift")
-        nc.scalar.copy(late_shift[:], spread[1][:])
+            spread_shift.append(bank)
+        late_shift = keep.tile([P, len(plain[1]), P], F32, name="late_shift")
+        nc.scalar.copy(late_shift[:], spread_shift[1][:])
         spread_wsum = psum.tile([P, PACK, P], F32, name="spread_wsum", tag="bank5")
         for t in range(PACK):
             nc.tensor.transpose(spread_wsum[:, t, :], wsum_cols[:, t : t + 1].to_broadcast([P, P]), ident[:])
-        offset_terms = {}
-        for b in SWAPPED + ADDED:
-            term = keep.tile([P, PACK, P], F32, name="swapped_term%d" % b, align_bytes=64)
-            nc.scalar.activation(term[:], spread_wsum[:], COPY, scale=factors[:, b, 1:2])
-            offset_terms[b] = term[:]
 
-        def make_terms(h):
-            terms = placed([P, len(groups[h]), PACK, P], F32, "offset_terms%d" % h, (SCALES + 2 * S + TABLE, WORDS0)[h])
+        terms = {}
+        for b in SWAPPED + ADDED:
+            term = keep.tile([P, PACK, P], F32, name="entry_term%d" % b, align_bytes=64)
+            nc.scalar.activation(term[:], spread_wsum[:], COPY, scale=factors[:, b, 1:2])
+            terms[b] = term[:]
+
+        def make_plain_terms(h):
+            tile = placed([P, len(plain[h]), PACK, P], F32, "plain_terms%d" % h, (EARLY_TERMS, WORDS0)[h])
             for t in range(PACK):
                 if h == 0:
-                    nc.scalar.activation(terms[:, :, t, :], spread[0][:], COPY, scale=wsum_cols[:, t : t + 1])
+                    nc.scalar.activation(tile[:, :, t, :], spread_shift[0][:], COPY, scale=wsum_cols[:, t : t + 1])
                 else:
-                    nc.vector.tensor_scalar(terms[:, :, t, :], late_shift[:], wsum_cols[:, t : t + 1], None, MULT)
-            for i, b in enumerate(groups[h]):
-                offset_terms[b] = terms[:, i, :, :]
+                    nc.vector.tensor_scalar(tile[:, :, t, :], late_shift[:], wsum_cols[:, t : t + 1], None, MULT)
+            for i, b in enumerate(plain[h]):
+                terms[b] = tile[:, i, :, :]
 
-        make_terms(0)
-        sums = {}
-        picked = {}
+        make_plain_terms(0)
+        sums, picked, turned, rounded = {}, {}, {}, {}
 
         def gather(o, h):
             codes = keep.tile([P, HALF], U32, name="x_codes%d_%d" % (o, h), align_bytes=64)
@@ -181,79 +190,83 @@ def tile_picked_zdq_linnone_po_kernel(
         out_words = out_1[0].rearrange("p j r -> p (j r)").bitcast(I32)
         out_plane = keep.tile([P, S], U8, name="out_plane", align_bytes=64)
         results = [keep.tile([P, PACK, CHUNK], F32, name="result%d" % c) for c in range(CHUNKS)]
-        rounded = {}
         scaled = [keep.tile([P, PACK, P], F32, name="scaled%d" % b, align_bytes=64) for b in range(BLOCKS)]
-
-        turned_banks = {}
 
         def scale(b):
             dealt = sums[b][:].rearrange("j (p t) -> j t p", t=PACK)
             if b in SWAPPED:
-                nc.vector.scalar_tensor_tensor(scaled[b][:], dealt, factors[:, b, 0:1], offset_terms[b], MULT, ADD)
+                nc.vector.scalar_tensor_tensor(scaled[b][:], dealt, factors[:, b, 0:1], terms[b], MULT, ADD)
             else:
                 nc.scalar.activation(scaled[b][:], dealt, COPY, scale=factors[:, b, 0:1])
 
         def finish(b):
-            turned = turned_banks[b] = psum.tile([P, PACK, P], F32, name="turned%d" % b, tag="bank%d" % b)
+            bank = turned[b] = psum.tile([P, PACK, P], F32, name="turned%d" % b, tag="bank%d" % b)
             for t in range(PACK):
                 if b in ADDED:
-                    nc.tensor.matmul(turned[:, t, :], offset_terms[b][:, t, :], ident[:], start=True, stop=False, is_transpose=True)
-                    nc.tensor.matmul(turned[:, t, :], scaled[b][:, t, :], ident[:], start=False, stop=True, is_transpose=True)
+                    nc.tensor.matmul(bank[:, t, :], terms[b][:, t, :], ident[:], start=True, stop=False, is_transpose=True)
+                    nc.tensor.matmul(bank[:, t, :], scaled[b][:, t, :], ident[:], start=False, stop=True, is_transpose=True)
                 else:
-                    nc.tensor.transpose(turned[:, t, :], scaled[b][:, t, :], ident[:])
+                    nc.tensor.transpose(bank[:, t, :], scaled[b][:, t, :], ident[:])
             c, i = divmod(b, 2)
+            result = results[c][:, :, P * i : P * (i + 1)]
             if b in SWAPPED + ADDED:
-                nc.scalar.copy(results[c][:, :, P * i : P * (i + 1)], turned[:])
+                nc.scalar.copy(result, bank[:])
             else:
-                nc.vector.tensor_tensor(results[c][:, :, P * i : P * (i + 1)], turned[:], offset_terms[b], ADD)
+                nc.vector.tensor_tensor(result, bank[:], terms[b], ADD)
             if c == 0:
-                nc.sync.dma_start(out_rows[:, :, P * b : P * (b + 1)], results[c][:, :, P * i : P * (i + 1)])
+                nc.sync.dma_start(out_rows[:, :, P * b : P * (b + 1)], result)
             elif i == 1:
                 nc.sync.dma_start(out_rows[:, :, CHUNK * c : CHUNK * (c + 1)], results[c][:])
 
-        def quantise(c):
-            tag = ("scaled5", "scaled7", "out_codes2", "out_codes3")[c]
-            codes = keep.tile([P, CHUNK], U32, name="out_codes%d" % c, tag=tag, align_bytes=64)
-            cols = slice(CHUNK * c, CHUNK * (c + 1))
-            nc.vector.quantize_mx(
-                out=codes[:].bitcast(FP8X4), scales=out_plane[:, cols], in_=rounded[c][:].rearrange("p j r -> p (j r)")
-            )
-            nc.sync.dma_start(out_words[:, cols], codes[:].bitcast(I32))
+        def round_block(b):
+            c, i = divmod(b, 2)
+            if i == 0:
+                tag = "x_codes1_1" if c == 1 else "rounded%d" % c
+                rounded[c] = keep.tile([P, CHUNK, PACK], BF16, name="rounded%d" % c, tag=tag, align_bytes=64)
+            dst = rounded[c][:, P * i : P * (i + 1), :]
+            result = results[c][:, :, P * i : P * (i + 1)]
+            if b in GPSIMD_ROUNDS:
+                nc.gpsimd.tensor_scalar(dst, result.rearrange("p t j -> p j t"), 1.0, -0.0, MULT, ADD)
+            elif b in SWAPPED:
+                nc.scalar.copy(dst, turned[b][:].rearrange("p t j -> p j t"))
+            else:
+                interleave(nc.vector.tensor_copy, dst, result)
+
+        def quantise(runs, tag):
+            first, last = runs[0][0], runs[-1][1]
+            codes = keep.tile([P, P * (last - first)], U32, name="out_codes%d" % first, tag=tag, align_bytes=64)
+            for lo, hi in runs:
+                c = lo // 2
+                nc.vector.quantize_mx(
+                    out=codes[:, P * (lo - first) : P * (hi - first)].bitcast(FP8X4),
+                    scales=out_plane[:, P * lo : P * hi],
+                    in_=rounded[c][:, P * (lo - 2 * c) : P * (hi - 2 * c), :].rearrange("p j r -> p (j r)"),
+                )
+            nc.sync.dma_start(out_words[:, P * first : P * last], codes[:].bitcast(I32))
 
         for h in range(2):
             gather(0, h)
-        make_terms(1)
+        make_plain_terms(1)
         for b in range(BLOCKS):
             multiply(0, b)
         for h in range(2):
             gather(1, h)
-        for b in range(4):
+        for b in range(BLOCKS // 2):
             multiply(1, b)
             scale(b)
         for c in range(CHUNKS):
             finish(2 * c)
             finish(2 * c + 1)
-            if c < 2:
-                for b in (2 * c + 4, 2 * c + 5):
+            if c < CHUNKS // 2:
+                for b in (2 * c + BLOCKS // 2, 2 * c + BLOCKS // 2 + 1):
                     multiply(1, b)
                     scale(b)
-        for c in range(CHUNKS):
-            tag = ("rounded0", "swapped_term7", "rounded2", "rounded3")[c]
-            rounded[c] = keep.tile([P, CHUNK, PACK], BF16, name="rounded%d" % c, tag=tag, align_bytes=64)
-            for i in range(2):
-                b = 2 * c + i
-                if c == 0 or b == 3:
-                    cols = slice(P * i, P * (i + 1))
-                    nc.gpsimd.tensor_scalar(
-                        rounded[c][:, cols, :], results[c][:, :, cols].rearrange("p t j -> p j t"), 1.0, -0.0, MULT, ADD
-                    )
-                elif b in SWAPPED:
-                    nc.scalar.copy(rounded[c][:, P * i : P * (i + 1), :], turned_banks[b][:].rearrange("p t j -> p j t"))
-                else:
-                    copy = nc.scalar.copy if b in SCALAR_ROUNDS else nc.vector.tensor_copy
-                    interleave(copy, rounded[c][:, P * i : P * (i + 1), :], results[c][:, :, P * i : P * (i + 1)])
-        for c in range(CHUNKS):
-            quantise(c)
+        for b in range(BLOCKS):
+            round_block(b)
+        quantise([(0, 2)], "scaled5")
+        quantise([(2, 4)], "scaled7")
+        quantise([(4, 6), (6, 7)], "out_codes4")
+        quantise([(7, 8)], "out_codes7")
         for q in range(4):
             queue = nc.sync if q % 2 == 0 else nc.scalar
             queue.dma_start(out_2[0, 4 * q : 4 * q + 4, :].bitcast(I32), out_plane[32 * q : 32 * q + 4, :].bitcast(I32))

@@ -68,7 +68,7 @@ def tile_picked_zdq_linnone_po_kernel(
         nc.sync.dma_start(wsum_cols[:], wsum.rearrange("(p t) o -> p (t o)", t=PACK))
         w_rows = w1.rearrange("(o p r) m -> o p r m", o=PASSES, r=PACK)
         w_raw = [keep.tile([P, PACK, N], F32, name="w_raw0", align_bytes=64)]
-        nc.sync.dma_start(w_raw[0][:], w_rows[0])
+        nc.scalar.dma_start(w_raw[0][:], w_rows[0])
 
         zero = keep.tile([P, 1], F32, name="zero")
         upper = slice(GAIN_ROW + 1, SHIFT_ROW)

@@ -26,8 +26,8 @@ HALF = S // 2
 CHUNK = 2 * P
 CHUNKS = S // CHUNK
 
-SWAPPED = (2, 7)
-ADDED = (6,)
+SWAPPED = (2, 5)
+ADDED = (7,)
 GPSIMD_ROUNDS = (0, 1, 3)
 
 GAIN_ROW = P // 2 - 1
@@ -221,13 +221,13 @@ def tile_picked_zdq_linnone_po_kernel(
         def round_block(b):
             c, i = divmod(b, 2)
             if i == 0:
-                tag = "x_codes1_1" if c == 1 else "rounded%d" % c
+                tag = "scaled6" if c == 2 else "rounded%d" % c
                 rounded[c] = keep.tile([P, CHUNK, PACK], BF16, name="rounded%d" % c, tag=tag, align_bytes=64)
             dst = rounded[c][:, P * i : P * (i + 1), :]
             result = results[c][:, :, P * i : P * (i + 1)]
             if b in GPSIMD_ROUNDS:
                 nc.gpsimd.tensor_scalar(dst, result.rearrange("p t j -> p j t"), 1.0, -0.0, MULT, ADD)
-            elif b in SWAPPED:
+            elif b in SWAPPED + ADDED:
                 nc.scalar.copy(dst, turned[b][:].rearrange("p t j -> p j t"))
             else:
                 interleave(nc.vector.tensor_copy, dst, result)
@@ -257,14 +257,14 @@ def tile_picked_zdq_linnone_po_kernel(
         for c in range(CHUNKS):
             finish(2 * c)
             finish(2 * c + 1)
-            if c < CHUNKS // 2:
-                for b in (2 * c + BLOCKS // 2, 2 * c + BLOCKS // 2 + 1):
+            if c == 1:
+                for b in range(BLOCKS // 2, BLOCKS):
                     multiply(1, b)
                     scale(b)
         for b in range(BLOCKS):
             round_block(b)
-        quantise([(0, 2)], "scaled5")
-        quantise([(2, 4)], "scaled7")
+        quantise([(0, 2)], "scaled7")
+        quantise([(2, 4)], "entry_term7")
         quantise([(4, 6), (6, 7)], "out_codes4")
         quantise([(7, 8)], "out_codes7")
         for q in range(4):

@@ -167,18 +167,19 @@ def tile_picked_zdq_linnone_po_kernel(
         make_plain_terms(0)
         sums, picked, turned, rounded = {}, {}, {}, {}
 
-        def gather(o, h):
-            codes = keep.tile([P, HALF], U32, name="x_codes%d_%d" % (o, h), align_bytes=64)
-            nc.vector.tensor_copy(codes[:], word_table[o][:].indirect(offsets[:, HALF * h // 16 : HALF * (h + 1) // 16]))
-            picked[o, h] = codes
+        def gather(o, first, count):
+            codes = keep.tile([P, count], U32, name="x_codes%d_%d" % (o, first), align_bytes=64)
+            nc.vector.tensor_copy(codes[:], word_table[o][:].indirect(offsets[:, first // 16 : (first + count) // 16]))
+            for b in range(first // P, (first + count) // P):
+                picked[o, b] = (codes, P * b - first)
 
         def multiply(o, b):
             if o == 0:
                 sums[b] = psum.tile([P, N], F32, name="sums%d" % b, tag="bank%d" % b)
-            h, i = divmod(b, BLOCKS // 2)
+            codes, at = picked[o, b]
             nc.tensor.matmul_mx(
                 out=sums[b][:],
-                lhsT=picked[o, h][:, P * i : P * (i + 1)].bitcast(FP8X4),
+                lhsT=codes[:, at : at + P].bitcast(FP8X4),
                 lhsT_scale=x_planes[o][4 * o :, P * b : P * (b + 1)],
                 rhs=w_codes[o][:].bitcast(FP8X4),
                 rhs_scale=w_planes[o][:],
@@ -245,12 +246,12 @@ def tile_picked_zdq_linnone_po_kernel(
             nc.sync.dma_start(out_words[:, P * first : P * last], codes[:].bitcast(I32))
 
         for h in range(2):
-            gather(0, h)
+            gather(0, HALF * h, HALF)
         make_plain_terms(1)
         for b in range(BLOCKS):
             multiply(0, b)
-        for h in range(2):
-            gather(1, h)
+        for c in range(CHUNKS):
+            gather(1, CHUNK * c, CHUNK)
         for b in range(BLOCKS // 2):
             multiply(1, b)
             scale(b)

@@ -26,9 +26,9 @@ HALF = S // 2
 CHUNK = 2 * P
 CHUNKS = S // CHUNK
 
-SWAPPED = (2, 5)
+SWAPPED = (1,)
 ADDED = (7,)
-GPSIMD_ROUNDS = (0, 1, 3)
+GPSIMD_ROUNDS = (0, 1, 2, 3)
 
 GAIN_ROW = P // 2 - 1
 SHIFT_ROW = P - 1
@@ -138,11 +138,11 @@ def tile_picked_zdq_linnone_po_kernel(
         plain = [[b for b in range(4 * h, 4 * h + 4) if b not in SWAPPED + ADDED] for h in range(2)]
         spread_shift = []
         for h in range(2):
-            bank = psum.tile([P, len(plain[h]), P], F32, name="spread_shift", tag="bank%d" % (6 + h))
+            bank = psum.tile([P, len(plain[h]) * P], F32, name="spread_shift", tag="bank%d" % (6 + h))
             for i, b in enumerate(plain[h]):
-                nc.tensor.transpose(bank[:, i, :], factors[:, b, 1:2].to_broadcast([P, P]), ident[:])
+                nc.tensor.transpose(bank[:, P * i : P * (i + 1)], factors[:, b, 1:2].to_broadcast([P, P]), ident[:])
             spread_shift.append(bank)
-        late_shift = keep.tile([P, len(plain[1]), P], F32, name="late_shift")
+        late_shift = keep.tile([P, len(plain[1]) * P], F32, name="late_shift")
         nc.scalar.copy(late_shift[:], spread_shift[1][:])
         spread_wsum = psum.tile([P, PACK, P], F32, name="spread_wsum", tag="bank5")
         for t in range(PACK):
@@ -155,20 +155,20 @@ def tile_picked_zdq_linnone_po_kernel(
             terms[b] = term[:]
 
         def make_plain_terms(h):
-            tile = placed([P, len(plain[h]), PACK, P], F32, "plain_terms%d" % h, (EARLY_TERMS, WORDS0)[h])
+            tile = placed([P, PACK, len(plain[h]) * P], F32, "plain_terms%d" % h, (EARLY_TERMS, WORDS0)[h])
             for t in range(PACK):
                 if h == 0:
-                    nc.scalar.activation(tile[:, :, t, :], spread_shift[0][:], COPY, scale=wsum_cols[:, t : t + 1])
+                    nc.scalar.activation(tile[:, t, :], spread_shift[0][:], COPY, scale=wsum_cols[:, t : t + 1])
                 else:
-                    nc.vector.tensor_scalar(tile[:, :, t, :], late_shift[:], wsum_cols[:, t : t + 1], None, MULT)
+                    nc.vector.tensor_scalar(tile[:, t, :], late_shift[:], wsum_cols[:, t : t + 1], None, MULT)
             for i, b in enumerate(plain[h]):
-                terms[b] = tile[:, i, :, :]
+                terms[b] = tile[:, :, P * i : P * (i + 1)]
 
         make_plain_terms(0)
         sums, picked, turned, rounded = {}, {}, {}, {}
 
-        def gather(o, first, count):
-            codes = keep.tile([P, count], U32, name="x_codes%d_%d" % (o, first), align_bytes=64)
+        def gather(o, first, count, tag):
+            codes = keep.tile([P, count], U32, name="x_codes%d_%d" % (o, first), tag=tag, align_bytes=64)
             nc.vector.tensor_copy(codes[:], word_table[o][:].indirect(offsets[:, first // 16 : (first + count) // 16]))
             for b in range(first // P, (first + count) // P):
                 picked[o, b] = (codes, P * b - first)
@@ -191,23 +191,30 @@ def tile_picked_zdq_linnone_po_kernel(
         out_words = out_1[0].rearrange("p j r -> p (j r)").bitcast(I32)
         out_plane = keep.tile([P, S], U8, name="out_plane", align_bytes=64)
         results = [keep.tile([P, PACK, CHUNK], F32, name="result%d" % c) for c in range(CHUNKS)]
-        scaled = [keep.tile([P, PACK, P], F32, name="scaled%d" % b, align_bytes=64) for b in range(BLOCKS)]
+        scaled = {}
 
         def scale(b):
+            scaled[b] = keep.tile([P, PACK, P], F32, name="scaled%d" % b, align_bytes=64)
             dealt = sums[b][:].rearrange("j (p t) -> j t p", t=PACK)
             if b in SWAPPED:
                 nc.vector.scalar_tensor_tensor(scaled[b][:], dealt, factors[:, b, 0:1], terms[b], MULT, ADD)
             else:
                 nc.scalar.activation(scaled[b][:], dealt, COPY, scale=factors[:, b, 0:1])
 
-        def finish(b):
-            bank = turned[b] = psum.tile([P, PACK, P], F32, name="turned%d" % b, tag="bank%d" % b)
-            for t in range(PACK):
-                if b in ADDED:
-                    nc.tensor.matmul(bank[:, t, :], terms[b][:, t, :], ident[:], start=True, stop=False, is_transpose=True)
-                    nc.tensor.matmul(bank[:, t, :], scaled[b][:, t, :], ident[:], start=False, stop=True, is_transpose=True)
-                else:
+        def turn(b):
+            if b in ADDED:
+                bank = turned[b] = psum.tile([P, PACK, P], F32, name="turned%d" % b, tag="bank0")
+                for n, source in enumerate((terms[b], scaled[b][:])):
+                    for t in range(PACK):
+                        first, last = n == 0 and t == 0, n == 1 and t == PACK - 1
+                        nc.tensor.matmul(bank[:, t, :], source[:, t, :], ident[:], start=first, stop=last, is_transpose=True)
+            else:
+                bank = turned[b] = psum.tile([P, PACK, P], F32, name="turned%d" % b, tag="bank%d" % b)
+                for t in range(PACK):
                     nc.tensor.transpose(bank[:, t, :], scaled[b][:, t, :], ident[:])
+
+        def finish(b):
+            bank = turned[b]
             c, i = divmod(b, 2)
             result = results[c][:, :, P * i : P * (i + 1)]
             if b in SWAPPED + ADDED:
@@ -219,55 +226,68 @@ def tile_picked_zdq_linnone_po_kernel(
             elif i == 1:
                 nc.sync.dma_start(out_rows[:, :, CHUNK * c : CHUNK * (c + 1)], results[c][:])
 
-        def round_block(b):
-            c, i = divmod(b, 2)
-            if i == 0:
-                tag = "scaled6" if c == 2 else "rounded%d" % c
-                rounded[c] = keep.tile([P, CHUNK, PACK], BF16, name="rounded%d" % c, tag=tag, align_bytes=64)
-            dst = rounded[c][:, P * i : P * (i + 1), :]
-            result = results[c][:, :, P * i : P * (i + 1)]
-            if b in GPSIMD_ROUNDS:
+        def round_block(b, engine):
+            h, i = divmod(b, 4)
+            if h not in rounded:
+                if h == 0:
+                    rounded[h] = placed([P, HALF, PACK], BF16, "rounded0", WORDS1)
+                else:
+                    rounded[h] = keep.tile([P, HALF, PACK], BF16, name="rounded1", tag="scaled6", align_bytes=64)
+            dst = rounded[h][:, P * i : P * (i + 1), :]
+            result = results[b // 2][:, :, P * (b % 2) : P * (b % 2 + 1)]
+            if engine == "gpsimd":
                 nc.gpsimd.tensor_scalar(dst, result.rearrange("p t j -> p j t"), 1.0, -0.0, MULT, ADD)
-            elif b in SWAPPED + ADDED:
+            elif b in ADDED:
                 nc.scalar.copy(dst, turned[b][:].rearrange("p t j -> p j t"))
             else:
-                interleave(nc.vector.tensor_copy, dst, result)
+                interleave(nc.vector.tensor_copy if engine == "vector" else nc.scalar.copy, dst, result)
 
-        def quantise(runs, tag):
-            first, last = runs[0][0], runs[-1][1]
-            codes = keep.tile([P, P * (last - first)], U32, name="out_codes%d" % first, tag=tag, align_bytes=64)
-            for lo, hi in runs:
-                c = lo // 2
-                nc.vector.quantize_mx(
-                    out=codes[:, P * (lo - first) : P * (hi - first)].bitcast(FP8X4),
-                    scales=out_plane[:, P * lo : P * hi],
-                    in_=rounded[c][:, P * (lo - 2 * c) : P * (hi - 2 * c), :].rearrange("p j r -> p (j r)"),
-                )
-            nc.sync.dma_start(out_words[:, P * first : P * last], codes[:].bitcast(I32))
+        def quantise(h):
+            codes = placed([P, HALF], U32, "out_codes%d" % h, WORDS0 + 4 * HALF * h)
+            nc.vector.quantize_mx(
+                out=codes[:].bitcast(FP8X4),
+                scales=out_plane[:, HALF * h : HALF * (h + 1)],
+                in_=rounded[h][:].rearrange("p j r -> p (j r)"),
+            )
+            nc.sync.dma_start(out_words[:, HALF * h : HALF * (h + 1)], codes[:].bitcast(I32))
 
         for h in range(2):
-            gather(0, HALF * h, HALF)
+            gather(0, HALF * h, HALF, "x_codes0_%d" % h)
         make_plain_terms(1)
         for b in range(BLOCKS):
             multiply(0, b)
-        for c in range(CHUNKS):
-            gather(1, CHUNK * c, CHUNK)
-        for b in range(BLOCKS // 2):
+        for c in range(2):
+            gather(1, CHUNK * c, CHUNK, "x_codes1_%d" % c)
+        for b in range(4):
             multiply(1, b)
             scale(b)
-        for c in range(CHUNKS):
-            finish(2 * c)
-            finish(2 * c + 1)
-            if c == 1:
-                for b in range(BLOCKS // 2, BLOCKS):
-                    multiply(1, b)
-                    scale(b)
-        for b in range(BLOCKS):
-            round_block(b)
-        quantise([(0, 2)], "scaled7")
-        quantise([(2, 4)], "entry_term7")
-        quantise([(4, 6), (6, 7)], "out_codes4")
-        quantise([(7, 8)], "out_codes7")
+        gather(1, CHUNK * 2, CHUNK, "entry_term1")
+        turn(0)
+        finish(0)
+        gather(1, CHUNK * 3, CHUNK, "scaled0")
+        turn(1)
+        finish(1)
+        turn(2)
+        finish(2)
+        for b in (4, 5):
+            multiply(1, b)
+            scale(b)
+        turn(3)
+        finish(3)
+        for b in (6, 7):
+            multiply(1, b)
+            scale(b)
+        for b in range(4, BLOCKS):
+            turn(b)
+            finish(b)
+        for b in GPSIMD_ROUNDS:
+            round_block(b, "gpsimd")
+        round_block(7, "scalar")
+        round_block(4, "scalar")
+        quantise(0)
+        round_block(5, "vector")
+        round_block(6, "vector")
+        quantise(1)
         for q in range(4):
             queue = nc.sync if q % 2 == 0 else nc.scalar
             queue.dma_start(out_2[0, 4 * q : 4 * q + 4, :].bitcast(I32), out_plane[32 * q : 32 * q + 4, :].bitcast(I32))

@@ -26,7 +26,7 @@ HALF = S // 2
 CHUNK = 2 * P
 CHUNKS = S // CHUNK
 
-SWAPPED = (1,)
+SWAPPED = ()
 ADDED = (7,)
 GPSIMD_ROUNDS = (0, 1, 2, 3)
 
@@ -242,52 +242,51 @@ def tile_picked_zdq_linnone_po_kernel(
             else:
                 interleave(nc.vector.tensor_copy if engine == "vector" else nc.scalar.copy, dst, result)
 
-        def quantise(h):
-            codes = placed([P, HALF], U32, "out_codes%d" % h, WORDS0 + 4 * HALF * h)
+        def quantise(first, last):
+            h = first // 4
+            codes = placed([P, P * (last - first)], U32, "out_codes%d" % first, WORDS0 + 4 * P * first)
             nc.vector.quantize_mx(
                 out=codes[:].bitcast(FP8X4),
-                scales=out_plane[:, HALF * h : HALF * (h + 1)],
-                in_=rounded[h][:].rearrange("p j r -> p (j r)"),
+                scales=out_plane[:, P * first : P * last],
+                in_=rounded[h][:, P * (first - 4 * h) : P * (last - 4 * h), :].rearrange("p j r -> p (j r)"),
             )
-            nc.sync.dma_start(out_words[:, HALF * h : HALF * (h + 1)], codes[:].bitcast(I32))
+            nc.sync.dma_start(out_words[:, P * first : P * last], codes[:].bitcast(I32))
 
         for h in range(2):
             gather(0, HALF * h, HALF, "x_codes0_%d" % h)
         make_plain_terms(1)
         for b in range(BLOCKS):
             multiply(0, b)
-        for c in range(2):
+        for c in range(CHUNKS):
             gather(1, CHUNK * c, CHUNK, "x_codes1_%d" % c)
         for b in range(4):
             multiply(1, b)
             scale(b)
-        gather(1, CHUNK * 2, CHUNK, "entry_term1")
         turn(0)
         finish(0)
-        gather(1, CHUNK * 3, CHUNK, "scaled0")
-        turn(1)
-        finish(1)
-        turn(2)
-        finish(2)
         for b in (4, 5):
             multiply(1, b)
             scale(b)
-        turn(3)
-        finish(3)
+        for b in (1, 2, 3):
+            turn(b)
+            finish(b)
         for b in (6, 7):
             multiply(1, b)
             scale(b)
-        for b in range(4, BLOCKS):
+        for b in (4, 5, 6):
             turn(b)
             finish(b)
+        turn(7)
         for b in GPSIMD_ROUNDS:
             round_block(b, "gpsimd")
-        round_block(7, "scalar")
         round_block(4, "scalar")
-        quantise(0)
-        round_block(5, "vector")
+        round_block(5, "scalar")
+        finish(7)
+        round_block(7, "scalar")
+        quantise(0, 4)
         round_block(6, "vector")
-        quantise(1)
+        quantise(4, 6)
+        quantise(6, 8)
         for q in range(4):
             queue = nc.sync if q % 2 == 0 else nc.scalar
             queue.dma_start(out_2[0, 4 * q : 4 * q + 4, :].bitcast(I32), out_plane[32 * q : 32 * q + 4, :].bitcast(I32))

@@ -30,11 +30,8 @@ SWAPPED = ()
 ADDED = (7,)
 GPSIMD_ROUNDS = (0, 1, 2, 3)
 
-GAIN_ROW = P // 2 - 1
-SHIFT_ROW = P - 1
-SCALAR_CLEARS = 2048
-VECTOR_CLEARS = 2560
-FIRST_CLEARED = 31
+HALF_STEP = 8
+EDGE = 32
 
 TABLE = 4 * T
 WORDS0 = TABLE + 16 * N
@@ -59,34 +56,34 @@ def tile_picked_zdq_linnone_po_kernel(
         def placed(shape, dtype, name, offset):
             return reuse.tile(shape, dtype, name=name, align_bytes=64, offset=offset)
 
-        row_table = placed([P, T], F32, "row_table", 0)
-        nc.sync.dma_start(row_table[GAIN_ROW : GAIN_ROW + 1, :], gain[0:1, :])
-        nc.sync.dma_start(row_table[SHIFT_ROW : SHIFT_ROW + 1, :], shift[0:1, :])
+        w_rows = w1.rearrange("(o p r) m -> o p r m", o=PASSES, r=PACK)
+        w_raw = [keep.tile([P, PACK, N], F32, name="w_raw0", align_bytes=64)]
+        nc.sync.dma_start(w_raw[0][:], w_rows[0])
         offsets = keep.tile([P, S // 16], U16, name="offsets")
         nc.sync.dma_start(offsets[:], offs)
         wsum_cols = keep.tile([P, PACK], F32, name="wsum_cols")
         nc.sync.dma_start(wsum_cols[:], wsum.rearrange("(p t) o -> p (t o)", t=PACK))
-        w_rows = w1.rearrange("(o p r) m -> o p r m", o=PASSES, r=PACK)
-        w_raw = [keep.tile([P, PACK, N], F32, name="w_raw0", align_bytes=64)]
-        nc.scalar.dma_start(w_raw[0][:], w_rows[0])
 
-        zero = keep.tile([P, 1], F32, name="zero")
-        upper = slice(GAIN_ROW + 1, SHIFT_ROW)
-        nc.gpsimd.memset(zero[upper, :], 0.0)
-        first_zero = placed([P, FIRST_CLEARED], F32, "first_zero", WORDS0 - 64)
-        nc.gpsimd.memset(first_zero[:GAIN_ROW, :], 0.0)
+        row_table = placed([P, T], F32, "row_table", 0)
+        first_zero = placed([P, EDGE], F32, "first_zero", WORDS0 - 4 * EDGE)
+        last_zero = placed([P, EDGE], F32, "last_zero", WORDS0)
+        zero = placed([P, 1], F32, "zero", WORDS0 + 4 * EDGE)
+        for tile in (zero, first_zero, last_zero):
+            nc.gpsimd.memset(tile[:], 0.0)
         scale_table = placed([P, T], U8, "scale_table", SCALES)
-        scale_words = scale_table[:].bitcast(I32)
-        nc.vector.memset(scale_words[:, 1:], 0)
-        nc.vector.memset(scale_words[:, :1], 0)
+        nc.vector.memset(scale_table[:].bitcast(I32), 0)
         nc.sync.dma_start(scale_table[::4, :].bitcast(I32), x_scales.rearrange("o q c -> (o q) c").bitcast(I32))
-        nc.vector.tensor_copy(row_table[:GAIN_ROW, :FIRST_CLEARED], first_zero[:GAIN_ROW, :])
-        nc.vector.memset(row_table[:GAIN_ROW, FIRST_CLEARED:VECTOR_CLEARS], 0.0)
+        nc.vector.tensor_copy(row_table[:, :EDGE], first_zero[:])
         w_raw.append(placed([P, PACK, N], F32, "w_raw1", TABLE))
         nc.sync.dma_start(w_raw[1][:], w_rows[1])
-        nc.scalar.copy(row_table[upper, :SCALAR_CLEARS], zero[upper, :].to_broadcast([GAIN_ROW, SCALAR_CLEARS]))
-        nc.gpsimd.memset(row_table[upper, SCALAR_CLEARS:], 0.0)
-        nc.gpsimd.memset(row_table[:GAIN_ROW, VECTOR_CLEARS:], 0.0)
+        nc.vector.memset(row_table[:, EDGE : T // 2 - EDGE], 0.0)
+        nc.vector.tensor_copy(row_table[:, T // 2 - EDGE : T // 2], last_zero[:])
+        nc.scalar.copy(row_table[:, T // 2 :], zero[:].to_broadcast([P, T // 2]))
+        for half in (1, 0):
+            columns = slice(T // 2 * half, T // 2 * (half + 1))
+            for n, rows in enumerate((gain, shift)):
+                partition = P // 2 * n + HALF_STEP * half
+                nc.sync.dma_start(row_table[partition : partition + 1, columns], rows[0:1, columns])
         ident = keep.tile([P, P], F32, name="ident")
         make_identity(nc, ident[:])
 
@@ -133,7 +130,8 @@ def tile_picked_zdq_linnone_po_kernel(
             for i in range(4):
                 b = 4 * g + i
                 nc.tensor.transpose(bank[:, i, :], picked_rows[:, P * b : P * (b + 1)], ident[:])
-            nc.vector.tensor_copy(factors[:, 4 * g : 4 * g + 4, :], bank[:, :, GAIN_ROW :: P // 2])
+            halves = bank[:].rearrange("j i (n c) -> j i n c", n=2)[:, :, :, : 2 * HALF_STEP : HALF_STEP]
+            nc.vector.tensor_reduce(factors[:, 4 * g : 4 * g + 4, :], halves, mybir.AxisListType.X, ADD)
 
         plain = [[b for b in range(4 * h, 4 * h + 4) if b not in SWAPPED + ADDED] for h in range(2)]
         spread_shift = []
@@ -242,14 +240,16 @@ def tile_picked_zdq_linnone_po_kernel(
             else:
                 interleave(nc.vector.tensor_copy if engine == "vector" else nc.scalar.copy, dst, result)
 
-        def quantise(first, last):
+        def quantise(*borders):
+            first, last = borders[0], borders[-1]
             h = first // 4
             codes = placed([P, P * (last - first)], U32, "out_codes%d" % first, WORDS0 + 4 * P * first)
-            nc.vector.quantize_mx(
-                out=codes[:].bitcast(FP8X4),
-                scales=out_plane[:, P * first : P * last],
-                in_=rounded[h][:, P * (first - 4 * h) : P * (last - 4 * h), :].rearrange("p j r -> p (j r)"),
-            )
+            for lo, hi in zip(borders, borders[1:]):
+                nc.vector.quantize_mx(
+                    out=codes[:, P * (lo - first) : P * (hi - first)].bitcast(FP8X4),
+                    scales=out_plane[:, P * lo : P * hi],
+                    in_=rounded[h][:, P * (lo - 4 * h) : P * (hi - 4 * h), :].rearrange("p j r -> p (j r)"),
+                )
             nc.sync.dma_start(out_words[:, P * first : P * last], codes[:].bitcast(I32))
 
         for h in range(2):
@@ -285,8 +285,8 @@ def tile_picked_zdq_linnone_po_kernel(
         round_block(7, "scalar")
         quantise(0, 4)
         round_block(6, "vector")
-        quantise(4, 6)
-        quantise(6, 8)
+        quantise(4, 6, 7)
+        quantise(7, 8)
         for q in range(4):
             queue = nc.sync if q % 2 == 0 else nc.scalar
             queue.dma_start(out_2[0, 4 * q : 4 * q + 4, :].bitcast(I32), out_plane[32 * q : 32 * q + 4, :].bitcast(I32))

@@ -61,8 +61,6 @@ def tile_picked_zdq_linnone_po_kernel(
         nc.sync.dma_start(w_raw[0][:], w_rows[0])
         offsets = keep.tile([P, S // 16], U16, name="offsets")
         nc.sync.dma_start(offsets[:], offs)
-        wsum_cols = keep.tile([P, PACK], F32, name="wsum_cols")
-        nc.sync.dma_start(wsum_cols[:], wsum.rearrange("(p t) o -> p (t o)", t=PACK))
 
         row_table = placed([P, T], F32, "row_table", 0)
         first_zero = placed([P, EDGE], F32, "first_zero", WORDS0 - 4 * EDGE)
@@ -76,6 +74,9 @@ def tile_picked_zdq_linnone_po_kernel(
         nc.vector.tensor_copy(row_table[:, :EDGE], first_zero[:])
         w_raw.append(placed([P, PACK, N], F32, "w_raw1", TABLE))
         nc.sync.dma_start(w_raw[1][:], w_rows[1])
+        wsum_row = keep.tile([P, N], F32, name="wsum_row")
+        nc.gpsimd.memset(wsum_row[:], 0.0)
+        nc.sync.dma_start(wsum_row[0:1, :], wsum.rearrange("m o -> o m"))
         nc.vector.memset(row_table[:, EDGE : T // 2 - EDGE], 0.0)
         nc.vector.tensor_copy(row_table[:, T // 2 - EDGE : T // 2], last_zero[:])
         nc.scalar.copy(row_table[:, T // 2 :], zero[:].to_broadcast([P, T // 2]))
@@ -86,6 +87,12 @@ def tile_picked_zdq_linnone_po_kernel(
                 nc.sync.dma_start(row_table[partition : partition + 1, columns], rows[0:1, columns])
         ident = keep.tile([P, P], F32, name="ident")
         make_identity(nc, ident[:])
+
+        turned_wsum = psum.tile([P, PACK, P], F32, name="turned_wsum", tag="bank2")
+        for t in range(PACK):
+            nc.tensor.transpose(turned_wsum[:, t, :], wsum_row[:, t::PACK], ident[:])
+        wsum_cols = keep.tile([P, PACK], F32, name="wsum_cols")
+        nc.scalar.copy(wsum_cols[:], turned_wsum[:, :, 0])
 
         picked_scales = keep.tile([P, S], U8, name="picked_scales")
         nc.vector.tensor_copy(picked_scales[:], scale_table[:].indirect(offsets[:]))

from contextlib import ExitStack

import concourse.mybir as mybir
from concourse.masks import make_identity

K, T, S, N = 1024, 4096, 1024, 512
FLOPS = 2 * K * N * S
BYTES = K * T + K * T // 32 + 4 * K * N + 2 * 4 * T + 4 * N + 2 * 128 * S // 16 + 4 * N * S + N * S + N * S // 32

F32 = mybir.dt.float32
BF16 = mybir.dt.bfloat16
I32 = mybir.dt.int32
U32 = mybir.dt.uint32
U16 = mybir.dt.uint16
U8 = mybir.dt.uint8
FP8X4 = mybir.dt.float8_e4m3fn_x4
MULT = mybir.AluOpType.mult
ADD = mybir.AluOpType.add
COPY = mybir.ActivationFunctionType.Copy

P = 128
PACK = 4
PASSES = K // (P * PACK)
BLOCKS = S // P
HALF = S // 2
CHUNK = 2 * P
CHUNKS = S // CHUNK

SWAPPED = ()
ADDED = (7,)
GPSIMD_ROUNDS = (0, 1, 2, 3)

HALF_STEP = 8
EDGE = 32

TABLE = 4 * T
WORDS0 = TABLE + 16 * N
SCALES = WORDS0 + TABLE + 2 * S
WORDS1 = SCALES + 2 * S
EARLY_TERMS = WORDS1 + TABLE


def interleave(copy, dst, src):
    copy(out=dst.rearrange("p (c i) r -> p c r i", i=4), in_=src.rearrange("p r (c i) -> p c r i", i=4))


def tile_picked_zdq_linnone_po_kernel(
    tc, x_words, x_scales, w1, gain, shift, wsum, offs, out_0, out_1, out_2
):
    nc = tc.nc
    with ExitStack() as ctx:
        keep = ctx.enter_context(tc.tile_pool(name="keep", bufs=1))
        reuse = ctx.enter_context(tc.tile_pool(name="reuse", bufs=1))
        psum = ctx.enter_context(tc.psum_pool(name="psum", bufs=1))

        def placed(shape, dtype, name, offset):
            return reuse.tile(shape, dtype, name=name, align_bytes=64, offset=offset)

        w_rows = w1.rearrange("(o p r) m -> o p r m", o=PASSES, r=PACK)
        w_raw = [keep.tile([P, PACK, N], F32, name="w_raw0", align_bytes=64)]
        nc.sync.dma_start(w_raw[0][:], w_rows[0])
        offsets = keep.tile([P, S // 16], U16, name="offsets")
        nc.sync.dma_start(offsets[:], offs)

        row_table = placed([P, T], F32, "row_table", 0)
        first_zero = placed([P, EDGE], F32, "first_zero", WORDS0 - 4 * EDGE)
        last_zero = placed([P, EDGE], F32, "last_zero", WORDS0)
        zero = placed([P, 1], F32, "zero", WORDS0 + 4 * EDGE)
        for tile in (zero, first_zero, last_zero):
            nc.gpsimd.memset(tile[:], 0.0)
        scale_table = placed([P, T], U8, "scale_table", SCALES)
        nc.vector.memset(scale_table[:].bitcast(I32), 0)
        nc.sync.dma_start(scale_table[::4, :].bitcast(I32), x_scales.rearrange("o q c -> (o q) c").bitcast(I32))
        nc.vector.tensor_copy(row_table[:, :EDGE], first_zero[:])
        w_raw.append(placed([P, PACK, N], F32, "w_raw1", TABLE))
        nc.sync.dma_start(w_raw[1][:], w_rows[1])
        wsum_row = keep.tile([P, N], F32, name="wsum_row")
        nc.gpsimd.memset(wsum_row[:], 0.0)
        nc.sync.dma_start(wsum_row[0:1, :], wsum.rearrange("m o -> o m"))
        nc.vector.memset(row_table[:, EDGE : T // 2 - EDGE], 0.0)
        nc.vector.tensor_copy(row_table[:, T // 2 - EDGE : T // 2], last_zero[:])
        nc.scalar.copy(row_table[:, T // 2 :], zero[:].to_broadcast([P, T // 2]))
        for half in (1, 0):
            columns = slice(T // 2 * half, T // 2 * (half + 1))
            for n, rows in enumerate((gain, shift)):
                partition = P // 2 * n + HALF_STEP * half
                nc.sync.dma_start(row_table[partition : partition + 1, columns], rows[0:1, columns])
        ident = keep.tile([P, P], F32, name="ident")
        make_identity(nc, ident[:])

        turned_wsum = psum.tile([P, PACK, P], F32, name="turned_wsum", tag="bank2")
        for t in range(PACK):
            nc.tensor.transpose(turned_wsum[:, t, :], wsum_row[:, t::PACK], ident[:])
        wsum_cols = keep.tile([P, PACK], F32, name="wsum_cols")
        nc.scalar.copy(wsum_cols[:], turned_wsum[:, :, 0])

        picked_scales = keep.tile([P, S], U8, name="picked_scales")
        nc.vector.tensor_copy(picked_scales[:], scale_table[:].indirect(offsets[:]))
        word_table, x_planes = [], []

        def place_scales(o):
            plane = keep.tile([P, S], U8, name="x_plane%d" % o, tag=("x_plane0", "w_grouped0")[o], align_bytes=64)
            (nc.gpsimd, nc.vector)[o].memset(plane[:].bitcast(I32), 0)
            x_planes.append(plane)
            for i in range(4):
                nc.sync.dma_start(
                    plane[4 * o + i :: 32, :].bitcast(I32),
                    picked_scales[64 * o + 4 * i : 64 * (o + 1) : 16, :].bitcast(I32),
                )

        for o in range(PASSES):
            table = placed([P, T], U32, "word_table%d" % o, (WORDS0, WORDS1)[o])
            nc.sync.dma_start(table[:].bitcast(I32), x_words[o].rearrange("p c r -> p (c r)").bitcast(I32))
            word_table.append(table)
            if o == 0:
                place_scales(0)

        picked_rows = placed([P, S], F32, "picked_rows", SCALES - 2 * S)
        nc.vector.tensor_copy(picked_rows[:], row_table[:].indirect(offsets[:]))

        w_codes, w_planes = [], []
        for o in range(PASSES):
            grouped = keep.tile([P, N, PACK], BF16, name="w_grouped%d" % o, align_bytes=64)
            interleave(nc.scalar.copy, grouped[:], w_raw[o][:])
            codes = placed([P, N], U32, "w_codes%d" % o, (4 * N, 0)[o])
            plane = keep.tile([P, N], U8, name="w_plane%d" % o, align_bytes=64)
            nc.vector.quantize_mx(
                out=codes[:].bitcast(FP8X4), scales=plane[:], in_=grouped[:].rearrange("p m r -> p (m r)")
            )
            w_codes.append(codes)
            w_planes.append(plane)
        place_scales(1)

        factors = placed([P, BLOCKS, 2], F32, "factors", TABLE)
        for g in range(BLOCKS // 4):
            bank = psum.tile([P, 4, P], F32, name="turned_rows", tag="bank%d" % g)
            for i in range(4):
                b = 4 * g + i
                nc.tensor.transpose(bank[:, i, :], picked_rows[:, P * b : P * (b + 1)], ident[:])
            halves = bank[:].rearrange("j i (n c) -> j i n c", n=2)[:, :, :, : 2 * HALF_STEP : HALF_STEP]
            nc.vector.tensor_reduce(factors[:, 4 * g : 4 * g + 4, :], halves, mybir.AxisListType.X, ADD)

        plain = [[b for b in range(4 * h, 4 * h + 4) if b not in SWAPPED + ADDED] for h in range(2)]
        spread_shift = []
        for h in range(2):
            bank = psum.tile([P, len(plain[h]) * P], F32, name="spread_shift", tag="bank%d" % (6 + h))
            for i, b in enumerate(plain[h]):
                nc.tensor.transpose(bank[:, P * i : P * (i + 1)], factors[:, b, 1:2].to_broadcast([P, P]), ident[:])
            spread_shift.append(bank)
        late_shift = keep.tile([P, len(plain[1]) * P], F32, name="late_shift")
        nc.scalar.copy(late_shift[:], spread_shift[1][:])
        spread_wsum = psum.tile([P, PACK, P], F32, name="spread_wsum", tag="bank5")
        for t in range(PACK):
            nc.tensor.transpose(spread_wsum[:, t, :], wsum_cols[:, t : t + 1].to_broadcast([P, P]), ident[:])

        terms = {}
        for b in SWAPPED + ADDED:
            term = keep.tile([P, PACK, P], F32, name="entry_term%d" % b, align_bytes=64)
            nc.scalar.activation(term[:], spread_wsum[:], COPY, scale=factors[:, b, 1:2])
            terms[b] = term[:]

        def make_plain_terms(h):
            tile = placed([P, PACK, len(plain[h]) * P], F32, "plain_terms%d" % h, (EARLY_TERMS, WORDS0)[h])
            for t in range(PACK):
                if h == 0:
                    nc.scalar.activation(tile[:, t, :], spread_shift[0][:], COPY, scale=wsum_cols[:, t : t + 1])
                else:
                    nc.vector.tensor_scalar(tile[:, t, :], late_shift[:], wsum_cols[:, t : t + 1], None, MULT)
            for i, b in enumerate(plain[h]):
                terms[b] = tile[:, :, P * i : P * (i + 1)]

        make_plain_terms(0)
        sums, picked, turned, rounded = {}, {}, {}, {}

        def gather(o, first, count, tag):
            codes = keep.tile([P, count], U32, name="x_codes%d_%d" % (o, first), tag=tag, align_bytes=64)
            nc.vector.tensor_copy(codes[:], word_table[o][:].indirect(offsets[:, first // 16 : (first + count) // 16]))
            for b in range(first // P, (first + count) // P):
                picked[o, b] = (codes, P * b - first)

        def multiply(o, b):
            if o == 0:
                sums[b] = psum.tile([P, N], F32, name="sums%d" % b, tag="bank%d" % b)
            codes, at = picked[o, b]
            nc.tensor.matmul_mx(
                out=sums[b][:],
                lhsT=codes[:, at : at + P].bitcast(FP8X4),
                lhsT_scale=x_planes[o][4 * o :, P * b : P * (b + 1)],
                rhs=w_codes[o][:].bitcast(FP8X4),
                rhs_scale=w_planes[o][:],
                start=(o == 0),
                stop=(o == PASSES - 1),
            )

        out_rows = out_0.rearrange("(p t) j -> p t j", t=PACK)
        out_words = out_1[0].rearrange("p j r -> p (j r)").bitcast(I32)
        out_plane = keep.tile([P, S], U8, name="out_plane", align_bytes=64)
        results = [keep.tile([P, PACK, CHUNK], F32, name="result%d" % c) for c in range(CHUNKS)]
        scaled = {}

        def scale(b):
            scaled[b] = keep.tile([P, PACK, P], F32, name="scaled%d" % b, align_bytes=64)
            dealt = sums[b][:].rearrange("j (p t) -> j t p", t=PACK)
            if b in SWAPPED:
                nc.vector.scalar_tensor_tensor(scaled[b][:], dealt, factors[:, b, 0:1], terms[b], MULT, ADD)
            else:
                nc.scalar.activation(scaled[b][:], dealt, COPY, scale=factors[:, b, 0:1])

        def turn(b):
            if b in ADDED:
                bank = turned[b] = psum.tile([P, PACK, P], F32, name="turned%d" % b, tag="bank0")
                for n, source in enumerate((terms[b], scaled[b][:])):
                    for t in range(PACK):
                        first, last = n == 0 and t == 0, n == 1 and t == PACK - 1
                        nc.tensor.matmul(bank[:, t, :], source[:, t, :], ident[:], start=first, stop=last, is_transpose=True)
            else:
                bank = turned[b] = psum.tile([P, PACK, P], F32, name="turned%d" % b, tag="bank%d" % b)
                for t in range(PACK):
                    nc.tensor.transpose(bank[:, t, :], scaled[b][:, t, :], ident[:])

        def finish(b):
            bank = turned[b]
            c, i = divmod(b, 2)
            result = results[c][:, :, P * i : P * (i + 1)]
            if b in SWAPPED + ADDED:
                nc.scalar.copy(result, bank[:])
            else:
                nc.vector.tensor_tensor(result, bank[:], terms[b], ADD)
            if c == 0:
                nc.sync.dma_start(out_rows[:, :, P * b : P * (b + 1)], result)
            elif i == 1:
                nc.sync.dma_start(out_rows[:, :, CHUNK * c : CHUNK * (c + 1)], results[c][:])

        def round_block(b, engine):
            h, i = divmod(b, 4)
            if h not in rounded:
                if h == 0:
                    rounded[h] = placed([P, HALF, PACK], BF16, "rounded0", WORDS1)
                else:
                    rounded[h] = keep.tile([P, HALF, PACK], BF16, name="rounded1", tag="scaled6", align_bytes=64)
            dst = rounded[h][:, P * i : P * (i + 1), :]
            result = results[b // 2][:, :, P * (b % 2) : P * (b % 2 + 1)]
            if engine == "gpsimd":
                nc.gpsimd.tensor_scalar(dst, result.rearrange("p t j -> p j t"), 1.0, -0.0, MULT, ADD)
            elif b in ADDED:
                nc.scalar.copy(dst, turned[b][:].rearrange("p t j -> p j t"))
            else:
                interleave(nc.vector.tensor_copy if engine == "vector" else nc.scalar.copy, dst, result)

        def quantise(*borders):
            first, last = borders[0], borders[-1]
            h = first // 4
            codes = placed([P, P * (last - first)], U32, "out_codes%d" % first, WORDS0 + 4 * P * first)
            for lo, hi in zip(borders, borders[1:]):
                nc.vector.quantize_mx(
                    out=codes[:, P * (lo - first) : P * (hi - first)].bitcast(FP8X4),
                    scales=out_plane[:, P * lo : P * hi],
                    in_=rounded[h][:, P * (lo - 4 * h) : P * (hi - 4 * h), :].rearrange("p j r -> p (j r)"),
                )
            nc.sync.dma_start(out_words[:, P * first : P * last], codes[:].bitcast(I32))

        for h in range(2):
            gather(0, HALF * h, HALF, "x_codes0_%d" % h)
        make_plain_terms(1)
        for b in range(BLOCKS):
            multiply(0, b)
        for c in range(CHUNKS):
            gather(1, CHUNK * c, CHUNK, "x_codes1_%d" % c)
        for b in range(4):
            multiply(1, b)
            scale(b)
        turn(0)
        finish(0)
        for b in (4, 5):
            multiply(1, b)
            scale(b)
        for b in (1, 2, 3):
            turn(b)
            finish(b)
        for b in (6, 7):
            multiply(1, b)
            scale(b)
        for b in (4, 5, 6):
            turn(b)
            finish(b)
        turn(7)
        for b in GPSIMD_ROUNDS:
            round_block(b, "gpsimd")
        round_block(4, "scalar")
        round_block(5, "scalar")
        finish(7)
        round_block(7, "scalar")
        quantise(0, 4)
        round_block(6, "vector")
        quantise(4, 6, 7)
        quantise(7, 8)
        for q in range(4):
            queue = nc.sync if q % 2 == 0 else nc.scalar
            queue.dma_start(out_2[0, 4 * q : 4 * q + 4, :].bitcast(I32), out_plane[32 * q : 32 * q + 4, :].bitcast(I32))
